import numpy as np, ml_dtypes
CORES = [35,38,43,46]
N = 4
import mx_ref
BF = ml_dtypes.bfloat16
def cols(t, e):
    v = np.concatenate([t.reshape(128, -1, 4), np.zeros((128, 1, 4), BF)], axis=1)
    return np.ascontiguousarray(v[:, e]).reshape(128, -1)
def f(rng, *shape):
    return mx_ref.flush((rng.standard_normal(shape, dtype=np.float32) * np.exp2(rng.integers(-2, 3, shape[:-1] + (1,)))).astype(BF))
def wide(rng, *shape, cols=0):
    v = rng.standard_normal(shape, dtype=np.float32) * np.exp2(rng.integers(-12, 13, shape)).astype(np.float32)
    if cols: v *= np.repeat(np.exp2(rng.integers(-cols, cols + 1, shape[:-2] + (1, shape[-1] // 4))) * (rng.random(shape[:-2] + (1, shape[-1] // 4)) > 0.0625), 4, axis=-1).astype(np.float32)
    return mx_ref.flush(v.astype(BF))
T, NBIT, K, O = 384, 9, 512, 2
def planes(rng):
    v = np.zeros((N, 128, 512), BF); v[:, :, :4 * NBIT] = f(rng, N, 128, 4 * NBIT); return v
def setup_inputs(rng):
    return {"x": f(rng, N, 128, 4 * T), "hp": planes(rng), "e": f(rng, N, 128, 4 * K), "qw": f(rng, N, 128, O * 512)}
def setup_inputs_zero(rng):
    d = setup_inputs(rng)
    for r in rng.permutation(N)[:N // 2]:
        i = rng.integers(0, NBIT); d["hp"][r, :, 4 * i:4 * i + 4] = 0
    for r in range(N):
        for j in rng.permutation(T)[:T // 8]: d["x"][r, :, 4 * j:4 * j + 4] = 0
    return d
def setup_inputs_onebucket(rng):
    d = setup_inputs(rng); d["x"] = np.tile(d["hp"][rng.integers(0, N)][:, :4], (N, 1, T)); return d
def setup_inputs_all(rng):
    d = setup_inputs(rng); g = f(rng, 128, 4).astype(np.float32)[None, :, None, :]
    d["hp"][:, :, :4 * NBIT] = (g * np.exp2(rng.integers(0, 4, (N, 1, NBIT, 1)))).reshape(N, 128, -1).astype(BF)
    s = np.stack([rng.permutation(T) % 2 * 2 - 1 for r in range(N)]) * np.exp2(rng.integers(0, 4, (N, T)))
    d["x"] = (g * s[:, None, :, None]).reshape(N, 128, -1).astype(BF); return d
def setup_inputs_small(rng):
    d = setup_inputs(rng)
    for k in ("x", "hp"):
        v = d[k].astype(np.float32) * np.float32(2.0 ** -24)
        d[k] = mx_ref.flush(np.where(np.abs(v) < np.float32(2.0 ** -30), np.float32(0), v).astype(BF))
    return d
def setup_inputs_spread(rng):
    d = setup_inputs(rng); d["x"] = wide(rng, N, 128, 4 * T, cols=8); d["e"] = wide(rng, N, 128, 4 * K, cols=8); return d
def check_inputs(d):
    b = []
    if (np.asarray(d["hp"]).astype(np.float32)[:, :, 4 * NBIT:] != 0).any(): b.append("hp")
    return b
def reference(x, hp, e, qw):
    X = [mx_ref.quantize(x[r]) for r in range(N)]
    H = [mx_ref.quantize(hp[q]) for q in range(N)]
    W = [[mx_ref.quantize(np.ascontiguousarray(qw[r][:, 512 * o:512 * o + 512])) for o in range(O)] for r in range(N)]
    y = np.zeros((N, 128, N * O * T), np.float32); bk = np.zeros((N, N, T), np.float32)
    for r in range(N):
        for q in range(N):
            s = mx_ref.matmul(H[q], X[r])
            b = np.zeros(T, int)
            for i in range(NBIT): b += 2 ** i * (s[i] > 0)
            bk[r, q] = b
            c = mx_ref.quantize(cols(e[q], b))
            for o in range(O):
                k = (q * O + o) * T
                y[r][:, k:k + T] = mx_ref.matmul(W[r][o], c)
    return {"y": y, "bk": bk}

@@ -1,0 +1,294 @@
+from concourse.bass import DstId, RemoteDMATransfer
+from concourse.mybir import dt, AluOpType, ActivationFunctionType
+
+TOK, NBIT, KCOL, OUT = 384, 9, 512, 2
+SLOT = 10
+BLK = 32
+HPC = 16
+LAND = 128
+ZFROM = LAND + 3 * SLOT
+OWN = LAND + 128
+HCOLS = OWN + 128
+HALF = KCOL // 2
+RUNS = TOK // 16
+FREE = RUNS * BLK
+SUB = TOK // 3
+PART = TOK // 2
+
+_X4 = "float8_e4m3fn_x4"
+SCRATCH = {
+    "hb": ("sbuf", [128, 512], "bfloat16"), "h4": ("sbuf", [128, 4 * LAND + 512], "bfloat16"),
+    "HQ": ("sbuf", [128, 128], _X4), "HQS": ("sbuf", [128, 128], "uint8"),
+    "xb": ("sbuf", [128, 4 * TOK], "bfloat16"),
+    "wb": ("sbuf", [128, 4 * 128 * OUT], "bfloat16"),
+    "eb": ("sbuf", [128, 4 * KCOL], "bfloat16"),
+    "HC": ("sbuf", [128, HCOLS], _X4), "HS": ("sbuf", [128, HCOLS], "uint8"),
+    "XC": ("sbuf", [128, TOK], _X4), "XS": ("sbuf", [128, TOK], "uint8"),
+    "WC": ("sbuf", [128, 128 * OUT], _X4), "WS": ("sbuf", [128, 128 * OUT], "uint8"),
+    "mul": ("sbuf", [128, FREE], "bfloat16"),
+    "bits0": ("sbuf", [128, SUB // 16, BLK], "bfloat16"), "tr0": ("sbuf", [128, 2 * SUB], "bfloat16"),
+    "sc0": ("sbuf", [128, 2 * SUB], "float32"),
+    "bits1": ("sbuf", [128, RUNS, BLK], "bfloat16"), "tr1": ("sbuf", [128, FREE], "bfloat16"),
+    "sc1": ("sbuf", [128, FREE], "float32"),
+    "bf": ("sbuf", [128, 4, BLK], "float32"), "tb": ("sbuf", [128, 4, BLK], "float32"),
+    "offo": ("sbuf", [128, RUNS], "uint16"), "offr": ("sbuf", [128, 3 * RUNS], "uint16"),
+    "yst": ("sbuf", [128, 4 * OUT * TOK], "float32"),
+}
+for _k in range(4):
+    SCRATCH["EC%d" % _k] = ("sbuf", [128, KCOL], _X4)
+    SCRATCH["ES%d" % _k] = ("sbuf", [128, KCOL], "uint8")
+    for _o in range(OUT):
+        SCRATCH["G%d%d" % (_k, _o)] = ("sbuf", [128, KCOL], "float32")
+for _k in range(8):
+    SCRATCH["p%d" % _k] = ("psum", [128, 512], "float32")
+
+SEMAPHORES = (["l_hp", "l_e0", "l_e1", "l_x", "l_w", "zc", "st", "st2", "sent", "hpin", "nbin", "m0", "m1", "d0", "d1",
+               "q_z", "q_hp", "q_h4", "q_e0", "q_e1", "q_x", "q_w", "k_z", "k_h", "h4c", "k_a", "k_mul", "k_bf",
+               "t_o", "t_r0", "t_r1", "bfc", "v_tb",
+               "bit0", "bit1", "bit2", "trn0", "trn1", "scn0", "scn1", "off0", "off1", "off2", "off3"]
+              + ["t%d%d" % (k, o) for k in range(4) for o in range(OUT)]
+              + ["c%d%d" % (k, o) for k in range(4) for o in range(OUT)]
+              + ["y%d%d" % (k, o) for k in range(4) for o in range(OUT)])
+
+
+def _bits(engines):
+    return sum(1 << e for e in engines)
+
+
+def rank_program(g, core, T, topo):
+    rank = T.rank_of(core)
+    if rank is None:
+        return
+    S = T.sem
+    cp = ActivationFunctionType.Copy
+    nb = mate = diag = None
+    for c in T.cores:
+        if c == core:
+            continue
+        if topo.chip(c) == topo.chip(core):
+            nb = c
+        elif topo.die(c) == topo.die(core):
+            mate = c
+        else:
+            diag = c
+    off = topo.engines(core, mate)
+    on = [e for e in topo.engines(core, nb) if e not in off]
+    oh = len(off) // 2
+    ranks = [rank, T.rank_of(nb), T.rank_of(mate), T.rank_of(diag)]
+    u8 = dt.uint8
+    sent = [0]
+
+    def cd(name, a, b):
+        return T[name][:, a:b].bitcast(u8)
+
+    def pl(name, a, b):
+        return T[name][:, a:b]
+
+    def send(*moves):
+        tr = []
+        for dst, eng, sem, src, out in moves:
+            a = topo.addr(dst)
+            tr.append(RemoteDMATransfer(dst_ids=[DstId(rid=a[0], pnc=a[1])], dma_engine_mask=_bits(eng),
+                                        remote_sem=S[sem], srcs=[src], dsts=[out]))
+            sent[0] += len(eng)
+        g.remote_dma_fused(tr, local_sem=S.sent)
+
+    y = g.sync
+    y.dma_start(T.eb[:, 0:4 * HALF], T.e[:, 0:4 * HALF]).then_inc(S.l_e0, 16)
+    y.dma_start(T.eb[:, 4 * HALF:], T.e[:, 4 * HALF:]).then_inc(S.l_e1, 16)
+    y.dma_start(T.wb[:, :], T.qw[:, :]).then_inc(S.l_w, 16)
+    a = g.scalar
+    a.dma_start(T.hb[:, 0:4 * HPC], T.hp[:, 0:4 * HPC]).then_inc(S.l_hp, 16)
+    a.dma_start(T.xb[:, :], T.x[:, :]).then_inc(S.l_x, 16)
+    nz = OWN - ZFROM
+    y.wait_ge(S.q_z, 1)
+    y.dma_start(cd("HC", ZFROM, OWN), cd("HC", 0, nz)).then_inc(S.zc, 16)
+    y.dma_start(pl("HS", ZFROM, OWN), pl("HS", 0, nz)).then_inc(S.zc, 16)
+
+    slots = [(nb, on, 0), (mate, off[:oh], 1), (diag, off[oh:], 2)]
+    g.wait_ge(S.q_hp, 1)
+    for view, src, name in ((cd, "HQ", "HC"), (pl, "HQS", "HS")):
+        send(*[(d, en, "hpin", view(src, 0, SLOT), view(name, LAND + SLOT * k, LAND + SLOT * (k + 1)))
+               for d, en, k in slots])
+    g.wait_ge(S.q_e0, 1)
+    send((mate, off, "m0", cd("EC0", 0, HALF), cd("EC2", 0, HALF)), (nb, on, "nbin", cd("EC0", 0, HALF), cd("EC1", 0, HALF)))
+    g.wait_ge(S.q_e1, 1)
+    send((mate, off, "m1", cd("EC0", HALF, KCOL), cd("EC2", HALF, KCOL)),
+         (nb, on, "nbin", cd("EC0", HALF, KCOL), cd("EC1", HALF, KCOL)))
+    send((mate, off, "m1", pl("ES0", 0, KCOL), pl("ES2", 0, KCOL)), (nb, on, "nbin", pl("ES0", 0, KCOL), pl("ES1", 0, KCOL)))
+    send((diag, off, "d1", cd("EC0", HALF, KCOL), cd("EC3", HALF, KCOL)))
+    send((diag, off, "d1", pl("ES0", 0, KCOL), pl("ES3", 0, KCOL)))
+    g.wait_ge(S.m0, len(off))
+    send((nb, on, "d0", cd("EC2", 0, HALF), cd("EC3", 0, HALF)))
+    g.wait_ge(S.sent, sent[0])
+
+    t = g.tensor
+
+    def planes(bank, moves, sem):
+        for i, (f, x0, n) in enumerate(moves):
+            m = t.matmul_mx(T[bank][:, 0:n], T.HC[:, f:f + 128], T.HS[:, f:f + 128], T.XC[:, x0:x0 + n], T.XS[:, x0:x0 + n],
+                            i == 0, i == len(moves) - 1)
+        m.then_inc(S[sem], 1)
+
+    def tables(k, banks):
+        for o in range(OUT):
+            w = slice(128 * o, 128 * o + 128)
+            t.matmul_mx(T[banks[o]][:, 0:KCOL], T.WC[:, w], T.WS[:, w], T["EC%d" % k][:, 0:KCOL], T["ES%d" % k][:, 0:KCOL],
+                        True, True).then_inc(S["t%d%d" % (k, o)], 1)
+
+    t.wait_ge(S.q_h4, 1)
+    t.wait_ge(S.q_x, 1)
+    t.wait_ge(S.q_z, 1)
+    t.wait_ge(S.zc, 32)
+    planes("p0", [(OWN - SLOT * s, SUB * s, SUB) for s in range(3)], "t_o")
+    t.wait_ge(S.q_e0, 1)
+    t.wait_ge(S.q_e1, 1)
+    t.wait_ge(S.q_w, 1)
+    tables(0, ("p2", "p3"))
+    t.wait_ge(S.hpin, 2 * (len(on) + 2 * oh))
+    for h in range(2):
+        planes(("p1", "p4")[h], [(LAND - BLK * b, PART * h, PART) for b in range(4)], "t_r%d" % h)
+    t.wait_ge(S.nbin, 3 * len(on))
+    tables(1, ("p5", "p6"))
+    t.wait_ge(S.m0, len(off))
+    t.wait_ge(S.m1, 2 * len(off))
+    t.wait_ge(S.bit0, 2)
+    tables(2, ("p7", "p0"))
+    t.wait_ge(S.c00, 1)
+    t.wait_ge(S.c01, 1)
+    t.wait_ge(S.d1, 2 * len(off))
+    t.wait_ge(S.d0, len(on))
+    tables(3, ("p2", "p3"))
+    bank = {(0, 0): "p2", (0, 1): "p3", (1, 0): "p5", (1, 1): "p6", (2, 0): "p7", (2, 1): "p0", (3, 0): "p2", (3, 1): "p3"}
+
+    def col(k, o):
+        c = (ranks[k] * OUT + o) * TOK
+        return slice(c, c + TOK)
+
+    def lst(k):
+        return T.offo[:, 0:RUNS] if k == 0 else T.offr[:, RUNS * (k - 1):RUNS * k]
+
+    def pick(k, o):
+        return T["G%d%d" % (k, o)][:, 0:KCOL].indirect(lst(k))
+
+    def list_made(q, k):
+        q.wait_ge(S["off%d" % k], 3 if k == 0 else 1)
+
+    v = g.vector
+    gt, mu, ad = AluOpType.is_gt, AluOpType.mult, AluOpType.add
+
+    def vcopy(k, o):
+        v.wait_ge(S["t%d%d" % (k, o)], 1)
+        v.tensor_copy(T["G%d%d" % (k, o)][:, 0:KCOL], T[bank[k, o]][:, 0:KCOL]).then_inc(S["c%d%d" % (k, o)], 1)
+
+    def vpick(k, o):
+        list_made(v, k)
+        v.wait_ge(S["c%d%d" % (k, o)], 1)
+        v.tensor_copy(T.yst[:, col(k, o)], pick(k, o)).then_inc(S["y%d%d" % (k, o)], 1)
+
+    def turn(p, n, sem, bt, r0, sb, tr, st):
+        r1 = r0 + n // 16
+        v.wait_ge(S[sem], 1)
+        for h in range(2):
+            v.tensor_scalar(bt[:, r0:r1, 16 * h:16 * h + 16], T[p][:, 0:n], 0.0, None, gt).then_inc(S[sb], 1)
+        v.wait_ge(S[sb], 2)
+        v.transpose(tr[:, BLK * r0:BLK * r1], bt[:, r0:r1, :]).then_inc(S[st], 1)
+
+    v.memset(T.h4[:, :], 0.0).then_inc(S.k_z, 1)
+    v.memset(T.hb[:, 4 * HPC:], 0.0).then_inc(S.k_h, 1)
+    v.wait_ge(S.k_z, 1)
+    v.quantize_mx(T.HC[:, 0:LAND], T.HS[:, 0:LAND], T.h4[:, 0:4 * LAND]).then_inc(S.q_z, 1)
+    v.memset(T.mul[:, :], 0.5).then_inc(S.k_a, 1)
+    v.wait_ge(S.k_a, 1)
+    for k in range(3):
+        v.memset(T.mul[:, SLOT * k:FREE:BLK], 0.0).then_inc(S.k_mul, 1)
+    v.memset(T.bf[0:BLK, :, :], 0.0).then_inc(S.k_bf, 1)
+    v.wait_ge(S.l_hp, 16)
+    v.wait_ge(S.k_h, 1)
+    v.quantize_mx(T.HQ[:, :], T.HQS[:, :], T.hb[:, :]).then_inc(S.q_hp, 1)
+    for h in range(2):
+        c = slice(HALF * h, HALF * h + HALF)
+        v.wait_ge(S["l_e%d" % h], 16)
+        v.quantize_mx(T.EC0[:, c], T.ES0[:, c], T.eb[:, 4 * HALF * h:4 * HALF * (h + 1)]).then_inc(S["q_e%d" % h], 1)
+        if h == 0:
+            v.wait_ge(S.h4c, 4)
+            v.quantize_mx(T.HC[:, OWN:], T.HS[:, OWN:], T.h4[:, 4 * LAND:]).then_inc(S.q_h4, 1)
+    v.wait_ge(S.l_x, 16)
+    v.quantize_mx(T.XC[:, :], T.XS[:, :], T.xb[:, :]).then_inc(S.q_x, 1)
+    v.wait_ge(S.l_w, 16)
+    v.quantize_mx(T.WC[:, :], T.WS[:, :], T.wb[:, :]).then_inc(S.q_w, 1)
+    v.wait_ge(S.k_mul, 3)
+    turn("p0", SUB, "t_o", T.bits0, 0, "bit0", T.tr0, "trn0")
+    v.wait_ge(S.trn0, 1)
+    v.tensor_tensor_scan(T.sc0[:, :], T.mul[:, 0:2 * SUB], T.tr0[:, :], 0.0, mu, ad).then_inc(S.scn0, 1)
+    v.wait_ge(S.scn0, 1)
+    q8 = SUB // 16
+    for s in range(3):
+        v.tensor_scalar(T.offo[:, q8 * s:q8 * (s + 1)], T.sc0[:, SLOT * s + NBIT - 1:2 * SUB:BLK], 256.0, None,
+                        mu).then_inc(S.off0, 1)
+    for h in range(2):
+        turn(("p1", "p4")[h], PART, "t_r%d" % h, T.bits1, RUNS // 2 * h, "bit%d" % (1 + h), T.tr1, "trn1")
+    v.wait_ge(S.trn1, 2)
+    v.tensor_tensor_scan(T.sc1[:, :], T.mul[:, :], T.tr1[:, :], 0.0, mu, ad).then_inc(S.scn1, 1)
+    v.wait_ge(S.scn1, 1)
+    for k in range(3):
+        v.tensor_scalar(T.offr[:, RUNS * k:RUNS * (k + 1)], T.sc1[:, SLOT * k + NBIT - 1:FREE:BLK], 256.0, None,
+                        mu).then_inc(S["off%d" % (k + 1)], 1)
+    vpick(1, 0)
+    v.wait_ge(S.k_bf, 1)
+    for k in (0, 2, 3):
+        list_made(v, k)
+    v.tensor_copy(T.bf[0:BLK, 0, 0:RUNS], T.offo[0:BLK, :]).then_inc(S.bfc, 1)
+    v.tensor_copy(T.bf[0:BLK, 1:4, 0:RUNS], T.offr[0:BLK, :]).then_inc(S.bfc, 1)
+    v.wait_ge(S.bfc, 2)
+    v.transpose(T.tb[0:BLK, :, :], T.bf[0:BLK, :, :]).then_inc(S.v_tb, 1)
+    vpick(2, 0)
+    vcopy(3, 0)
+    vpick(3, 0)
+
+    def acopy(k, o):
+        a.wait_ge(S["t%d%d" % (k, o)], 1)
+        a.activation(T["G%d%d" % (k, o)][:, 0:KCOL], T[bank[k, o]][:, 0:KCOL], cp).then_inc(S["c%d%d" % (k, o)], 1)
+
+    def apick(k, o):
+        list_made(a, k)
+        a.wait_ge(S["c%d%d" % (k, o)], 1)
+        a.activation(T.yst[:, col(k, o)], pick(k, o), cp).then_inc(S["y%d%d" % (k, o)], 1)
+
+    a.wait_ge(S.l_hp, 16)
+    a.wait_ge(S.k_z, 1)
+    for b in range(4):
+        f = 4 * (LAND + BLK * b)
+        a.activation(T.h4[:, f:f + 4 * HPC], T.hb[:, 0:4 * HPC], cp).then_inc(S.h4c, 1)
+    acopy(0, 0)
+    acopy(0, 1)
+    apick(0, 0)
+    apick(0, 1)
+    acopy(1, 0)
+    acopy(1, 1)
+    acopy(2, 0)
+    acopy(2, 1)
+    apick(1, 1)
+    apick(2, 1)
+    acopy(3, 1)
+    apick(3, 1)
+    a.wait_ge(S.y31, 1)
+    a.dma_start(T.y[:, col(3, 1)], T.yst[:, col(3, 1)]).then_inc(S.st2, 16)
+    a.wait_ge(S.st2, 16)
+
+    n = [0]
+
+    def store(k, o):
+        y.wait_ge(S["y%d%d" % (k, o)], 1)
+        y.dma_start(T.y[:, col(k, o)], T.yst[:, col(k, o)]).then_inc(S.st, 16)
+        n[0] += 16
+
+    for k, o in ((0, 0), (0, 1), (1, 0), (1, 1)):
+        store(k, o)
+    y.wait_ge(S.v_tb, 1)
+    for k in range(4):
+        y.dma_start(T.bk[ranks[k]:ranks[k] + 1, :], T.tb[0:RUNS, k, 0:16]).then_inc(S.st, 16)
+        n[0] += 16
+    for k, o in ((2, 0), (2, 1), (3, 0)):
+        store(k, o)
+    y.wait_ge(S.st, n[0])

@@ -1,40 +1,46 @@
 from concourse.bass import DstId, RemoteDMATransfer
 from concourse.mybir import dt, AluOpType, ActivationFunctionType
 
-TOK, NBIT, KCOL, OUT = 384, 9, 512, 2
-SLOT = 10
+TOK, NBIT, KCOL, OUT, NR = 384, 9, 512, 2, 4
 BLK = 32
+GRP = 16
+CH = TOK // BLK
+RUNS = TOK // GRP
+SET = NR * NBIT
+PER = 3
+BANKS = CH // PER
 HPC = 16
 LAND = 128
-ZFROM = LAND + 3 * SLOT
-OWN = LAND + 128
-HCOLS = OWN + 128
-HALF = KCOL // 2
-RUNS = TOK // 16
-FREE = RUNS * BLK
+OWN = LAND + 3 * NBIT
+TAIL = LAND + 48
+OWN4 = TAIL + 128
+SLOT = 10
 SUB = TOK // 3
-PART = TOK // 2
+HALF = KCOL // 2
+SCW = 2 * BLK * NBIT
 
 _X4 = "float8_e4m3fn_x4"
 SCRATCH = {
-    "hb": ("sbuf", [128, 512], "bfloat16"), "h4": ("sbuf", [128, 4 * LAND + 512], "bfloat16"),
+    "hb": ("sbuf", [128, 4 * HPC + 512], "bfloat16"), "h4": ("sbuf", [128, 512], "bfloat16"),
     "HQ": ("sbuf", [128, 128], _X4), "HQS": ("sbuf", [128, 128], "uint8"),
     "xb": ("sbuf", [128, 4 * TOK], "bfloat16"),
     "wb": ("sbuf", [128, 4 * 128 * OUT], "bfloat16"),
     "eb": ("sbuf", [128, 4 * KCOL], "bfloat16"),
-    "HC": ("sbuf", [128, HCOLS], _X4), "HS": ("sbuf", [128, HCOLS], "uint8"),
-    "XC": ("sbuf", [128, TOK], _X4), "XS": ("sbuf", [128, TOK], "uint8"),
+    "HC": ("sbuf", [128, OWN4 + 128], _X4), "HS": ("sbuf", [128, OWN4 + 128], "uint8"),
+    "XC": ("sbuf", [128, TOK + 128], _X4), "XS": ("sbuf", [128, TOK + 128], "uint8"),
     "WC": ("sbuf", [128, 128 * OUT], _X4), "WS": ("sbuf", [128, 128 * OUT], "uint8"),
-    "mul": ("sbuf", [128, FREE], "bfloat16"),
-    "bits0": ("sbuf", [128, SUB // 16, BLK], "bfloat16"), "tr0": ("sbuf", [128, 2 * SUB], "bfloat16"),
-    "sc0": ("sbuf", [128, 2 * SUB], "float32"),
-    "bits1": ("sbuf", [128, RUNS, BLK], "bfloat16"), "tr1": ("sbuf", [128, FREE], "bfloat16"),
-    "sc1": ("sbuf", [128, FREE], "float32"),
-    "bf": ("sbuf", [128, 4, BLK], "float32"), "tb": ("sbuf", [128, 4, BLK], "float32"),
-    "offo": ("sbuf", [128, RUNS], "uint16"), "offr": ("sbuf", [128, 3 * RUNS], "uint16"),
-    "yst": ("sbuf", [128, 4 * OUT * TOK], "float32"),
+    "mul": ("sbuf", [128, PER * SET], "bfloat16"), "bits": ("sbuf", [128, CH * SET], "bfloat16"),
+    "sc": ("sbuf", [128, SCW], "float32"), "turn": ("sbuf", [128, 2, 2, GRP], "float32"),
+    "mul0": ("sbuf", [128, 2 * SUB], "bfloat16"), "bits0": ("sbuf", [128, SUB // GRP, BLK], "bfloat16"),
+    "tr0": ("sbuf", [128, 2 * SUB], "bfloat16"), "sc0": ("sbuf", [128, 2 * SUB], "float16"),
+    "list0": ("sbuf", [128, RUNS], "uint16"),
+    "k0": ("sbuf", [128, BLK], "float32"), "k1": ("sbuf", [128, BLK], "float32"),
+    "k2": ("sbuf", [128, 8], "float32"), "k3": ("sbuf", [128, 8], "float32"), "k4": ("sbuf", [128, 8], "float32"),
+    "k5": ("sbuf", [128, 8], "float32"), "order": ("sbuf", [128, 8], "uint16"),
+    "lists": ("sbuf", [128, NR * BLK], "uint16"),
+    "yst": ("sbuf", [128, NR * OUT * TOK], "float32"),
 }
-for _k in range(4):
+for _k in range(NR):
     SCRATCH["EC%d" % _k] = ("sbuf", [128, KCOL], _X4)
     SCRATCH["ES%d" % _k] = ("sbuf", [128, KCOL], "uint8")
     for _o in range(OUT):
@@ -42,13 +48,20 @@ for _k in range(4):
 for _k in range(8):
     SCRATCH["p%d" % _k] = ("psum", [128, 512], "float32")
 
-SEMAPHORES = (["l_hp", "l_e0", "l_e1", "l_x", "l_w", "zc", "st", "st2", "sent", "hpin", "nbin", "m0", "m1", "d0", "d1",
-               "q_z", "q_hp", "q_h4", "q_e0", "q_e1", "q_x", "q_w", "k_z", "k_h", "h4c", "k_a", "k_mul", "k_bf",
-               "t_o", "t_r0", "t_r1", "bfc", "v_tb",
-               "bit0", "bit1", "bit2", "trn0", "trn1", "scn0", "scn1", "off0", "off1", "off2", "off3"]
-              + ["t%d%d" % (k, o) for k in range(4) for o in range(OUT)]
-              + ["c%d%d" % (k, o) for k in range(4) for o in range(OUT)]
-              + ["y%d%d" % (k, o) for k in range(4) for o in range(OUT)])
+CALLS = [["am", "an"], ["sm", "sn"], ["bm", "bn"], ["bd"], ["ar"], ["sr"]]
+SYNC = ["lh", "lx", "la", "lb", "lw", "y00", "y01", "bk", "y11", "y10", "y20", "y21", "y31"]
+TENSOR = ["mo", "m00", "m01", "mb0", "mb1", "mb2", "mb3", "m10a", "m11a", "m10b", "m11b", "m20a", "m21a", "m20b", "m21b",
+          "m30", "m31"]
+SCALAR = ["f0", "f1", "f2", "f3", "h4", "dc", "ds", "c00", "c01", "p00", "p01", "c10a", "c11a", "c20a", "c21a", "c21b",
+          "p11", "c30", "p21", "p30", "y30"]
+VECTOR = ["zh", "z0", "k1", "zs", "k2", "z1", "k3", "qh", "k4", "qx", "k5", "q4", "qa", "qb", "qw", "o0", "qy", "o1", "o2",
+          "o3", "g0", "g1", "u0", "g2", "u1", "g3", "u2", "u3", "c10b", "t1", "c11b", "t2", "c20b", "ls", "p10", "p20",
+          "c31", "p31"]
+BANK = {"mo": 7, "mb0": 4, "mb1": 5, "mb2": 6, "mb3": 7, "m00": 0, "m01": 1, "m10a": 2, "m11a": 3, "m10b": 4, "m11b": 5,
+        "m20a": 0, "m21a": 1, "m20b": 6, "m21b": 7, "m30": 2, "m31": 3}
+
+SEMAPHORES = (["sent", "planes", "parts", "st", "st2"] + [p + w for p in "abs" for w in "123"]
+              + [s + "_" for s in SYNC + TENSOR + SCALAR + VECTOR if s[0] != "y" and s != "bk"])
 
 
 def _bits(engines):
@@ -60,7 +73,8 @@ def rank_program(g, core, T, topo):
     if rank is None:
         return
     S = T.sem
-    cp = ActivationFunctionType.Copy
+    cp, ident = ActivationFunctionType.Copy, ActivationFunctionType.Identity
+    gt, lt, mu, ad = AluOpType.is_gt, AluOpType.is_lt, AluOpType.mult, AluOpType.add
     nb = mate = diag = None
     for c in T.cores:
         if c == core:
@@ -75,220 +89,184 @@ def rank_program(g, core, T, topo):
     on = [e for e in topo.engines(core, nb) if e not in off]
     oh = len(off) // 2
     ranks = [rank, T.rank_of(nb), T.rank_of(mate), T.rank_of(diag)]
-    u8 = dt.uint8
-    sent = [0]
+    slot = [3, 0, 1, 2]
+    y, a, v, t = g.sync, g.scalar, g.vector, g.tensor
+    zero = 4 * HPC
+    n3 = PER * SET
 
-    def cd(name, a, b):
-        return T[name][:, a:b].bitcast(u8)
+    def cd(name, c0, c1):
+        return T[name][:, c0:c1].bitcast(dt.uint8)
 
-    def pl(name, a, b):
-        return T[name][:, a:b]
+    def pl(name, c0, c1):
+        return T[name][:, c0:c1]
+
+    step = {}
+    far = {"planes": 2 * 3 * oh, "parts": 3}
+    far.update({p + k: len(off) for p in "abs" for k in "123"})
+
+    def load(out, src):
+        return [], lambda q: [q.dma_start(out, src)]
+
+    def quantise(needs, c, s, c0, c1, src):
+        return needs, lambda q: [q.quantize_mx(T[c][:, c0:c1], T[s][:, c0:c1], src)]
+
+    def move(q, out, src):
+        return q.tensor_copy(out, src) if q is v else q.activation(out, src, cp)
+
+    def products(bank, n, views):
+        def calls(q):
+            for i, (w, f, m, h) in enumerate(views):
+                last = q.matmul_mx(T["p%d" % bank][:, 0:n], T[w[0]][:, f:f + 128], T[w[1]][:, f:f + 128],
+                                   T[m[0]][:, h:h + n], T[m[1]][:, h:h + n], i == 0, i == len(views) - 1)
+            return [last]
+        return calls
+
+    H, X, W = ("HC", "HS"), ("XC", "XS"), ("WC", "WS")
+    step["lh"] = load(T.hb[:, 0:zero], T.hp[:, 0:zero])
+    step["la"] = load(T.eb[:, 0:4 * HALF], T.e[:, 0:4 * HALF])
+    step["lb"] = load(T.eb[:, 4 * HALF:], T.e[:, 4 * HALF:])
+    step["lw"] = load(T.wb[:, :], T.qw[:, :])
+    step["lx"] = load(T.xb[:, :], T.x[:, :])
+    step["zh"] = [], lambda q: [q.memset(T.hb[:, zero:], 0.0)]
+    step["zs"] = [], lambda q: [q.memset(T.sc[:, CH * SET:], 0.0)]
+    step["z0"] = quantise(["zh"], "HC", "HS", 0, LAND, T.hb[:, zero:])
+    step["z1"] = quantise(["zh"], "HC", "HS", TAIL, OWN4, T.hb[:, zero:])
+    step["qh"] = quantise(["zh", "lh"], "HQ", "HQS", 0, 128, T.hb[:, 0:512])
+    step["qa"] = quantise(["la"], "EC0", "ES0", 0, HALF, T.eb[:, 0:4 * HALF])
+    step["qb"] = quantise(["lb"], "EC0", "ES0", HALF, KCOL, T.eb[:, 4 * HALF:])
+    step["qw"] = quantise(["lw"], "WC", "WS", 0, 128 * OUT, T.wb[:, :])
+    step["qx"] = quantise(["lx"], "XC", "XS", 0, TOK, T.xb[:, :])
+    step["qy"] = quantise(["lx"], "XC", "XS", TOK, TOK + 128, T.xb[:, 0:512])
+    step["q4"] = quantise(["h4"], "HC", "HS", OWN4, OWN4 + 128, T.h4[:, :])
+    step["h4"] = ["zh", "lh"], lambda q: [move(q, T.h4[:, 4 * BLK * b:4 * BLK * (b + 1)], T.hb[:, 0:4 * BLK]) for b in range(4)]
+    step["dc"] = ["qh"], lambda q: [q.dma_start(cd("HC", OWN, TAIL), cd("HQ", 0, TAIL - OWN))]
+    step["ds"] = ["qh"], lambda q: [q.dma_start(pl("HS", OWN, TAIL), pl("HQS", 0, TAIL - OWN))]
+    step["f0"] = ["zh"], lambda q: [q.activation(T.mul[:, :], T.hb[:, zero:zero + n3], ident, bias=0.5)]
+    step["f1"] = ["zh"], lambda q: [q.activation(T.mul0[:, :], T.hb[:, zero:zero + 2 * SUB], ident, bias=0.5)]
+    step["f2"] = ["f0"], lambda q: [move(q, T.mul[:, 0::NBIT], T.hb[:, zero:zero + n3 // NBIT])]
+    step["f3"] = ["f1"], lambda q: [move(q, T.mul0[:, SLOT * s::BLK], T.hb[:, zero:zero + 2 * SUB // BLK]) for s in range(3)]
+    step["k1"] = ["parts"], lambda q: [q.transpose(T.k1[:, :], T.k0[:, :])]
+    step["k2"] = ["k1"], lambda q: [q.tensor_scalar(T.k3[:, :], T.k2[:, :], T.k1[:, 0:1], 0.125, ad, mu)]
+    step["k3"] = ["k2"], lambda q: [q.tensor_scalar(T.k4[:, :], T.k3[:, :], 0.0, float(CH * SET), lt, mu)]
+    step["k4"] = ["k3"], lambda q: [q.tensor_tensor(T.k5[:, :], T.k3[:, :], T.k4[:, :], ad)]
+    step["k5"] = ["k4"], lambda q: [q.tensor_copy(T.order[:, :], T.k5[:, :])]
+    po = T["p%d" % BANK["mo"]]
+    q8 = SUB // GRP
+    step["mo"] = ["qx", "z1", "q4"], products(BANK["mo"], SUB, [(H, OWN4 - SLOT * s, X, SUB * s) for s in range(3)])
+    step["o0"] = ["mo"], lambda q: [q.tensor_scalar(T.bits0[:, :, GRP * h:GRP * (h + 1)], po[:, 0:SUB], 0.0, 256.0, gt, mu)
+                                    for h in range(2)]
+    step["o1"] = ["o0"], lambda q: [q.transpose(T.tr0[:, :], T.bits0[:, :, :])]
+    step["o2"] = ["o1", "f3"], lambda q: [q.tensor_tensor_scan(T.sc0[:, :], T.mul0[:, :], T.tr0[:, :], 0.0, mu, ad)]
+    step["o3"] = ["o2"], lambda q: [q.tensor_copy(T.list0[:, q8 * s:q8 * (s + 1)], T.sc0[:, SLOT * s + NBIT - 1::BLK])
+                                    for s in range(3)]
+    readers = {"mo": ["o0"]}
+    for b in range(BANKS):
+        c = slice(n3 * b, n3 * (b + 1))
+        mb = "mb%d" % b
+        step[mb] = (["qx", "qy", "z0", "z1", "dc", "ds", "planes"],
+                    products(BANK[mb], 128, [(X, BLK * (PER * b + j), H, LAND - SET * j) for j in range(PER)]))
+        step["g%d" % b] = [mb], lambda q, c=c, mb=mb: [q.tensor_scalar(T.bits[:, c], T["p%d" % BANK[mb]][:, 0:n3], 0.0, 256.0, gt, mu)]
+        step["u%d" % b] = ["g%d" % b, "f2"], lambda q, c=c: [q.tensor_tensor_scan(T.sc[:, c], T.mul[:, :], T.bits[:, c], 0.0, mu, ad)]
+        readers[mb] = ["g%d" % b]
+    step["t1"] = (["zs"] + ["u%d" % b for b in range(BANKS)],
+                  lambda q: [q.transpose(T.turn[:, :, :, :], T.sc[:, NBIT - 1::NBIT])])
+    step["t2"] = ["t1"], lambda q: [q.transpose(T.sc[:, NBIT - 2::NBIT], T.turn[:, :, ::-1, :])]
+    step["ls"] = ["t2", "k5"], lambda q: [q.tensor_copy(T.lists[:, :], T.sc[:, 0:SCW].indirect(T.order[:, :]))]
+    first = BLK // NR * BLK
+    step["bk"] = ["t1"], lambda q: [q.dma_start(T.bk[ranks[j]:ranks[j] + 1, c], T.turn[slot[j]:e:NR, h, :, :])
+                                    for j in range(NR)
+                                    for h, c, e in ((0, slice(0, first), BLK), (1, slice(first, TOK), NR * CH - BLK))]
+    names = SYNC + TENSOR + SCALAR + VECTOR
+    part = {"": (0, 2), "a": (0, 1), "b": (1, 2)}
+    for s in names:
+        if s in step:
+            continue
+        what, k, o, (h0, h1) = s[0], int(s[1]), int(s[2]), part[s[3:]]
+        ko = s[1:3]
+        G = T["G" + ko]
+        c0 = (ranks[k] * OUT + o) * TOK
+        tok = slice(c0 + h0 * TOK // 2, c0 + h1 * TOK // 2)
+        if what == "m":
+            pieces = (s[3:] or "ab") + "s"
+            needs = ["qw"] + (["q" + p for p in pieces[:-1]] if k == 0 else [p + s[1] for p in pieces])
+            step[s] = needs, products(BANK[s], HALF * (h1 - h0), [(W, 128 * o, ("EC" + s[1], "ES" + s[1]), HALF * h0)])
+            readers[s] = [r for r in names if r.startswith("c" + s[1:])]
+        elif what == "c":
+            m = "m" + s[1:] if "m" + s[1:] in BANK else "m" + ko
+            f = HALF * h0 if m == "m" + ko else 0
+            src = T["p%d" % BANK[m]][:, f:f + HALF * (h1 - h0)]
+            other = "c" + ko + "a"
+            apart = f and (other in VECTOR) != (s in VECTOR)
+            step[s] = ([m] + [other] * apart,
+                       lambda q, G=G, src=src, h0=h0, h1=h1: [move(q, G[:, HALF * h0:HALF * h1], src)])
+        elif what == "p":
+            own = k == 0 and "o3" in names
+            f = 0 if own else BLK * slot[k]
+            lst = (T.list0 if own else T.lists)[:, f + h0 * RUNS // 2:f + h1 * RUNS // 2]
+            step[s] = (["o3" if own else "ls"] + [r for r in names if r.startswith("c" + ko)],
+                       lambda q, G=G, tok=tok, lst=lst: [move(q, T.yst[:, tok], G[:, 0:KCOL].indirect(lst))])
+        else:
+            step[s] = ([r for r in names if r.startswith("p" + s[1:])],
+                       lambda q, tok=tok: [q.dma_start(T.y[:, tok], T.yst[:, tok])])
+    held = {}
+    for s in TENSOR:
+        step[s][0].extend(held.get(BANK[s], []))
+        held[BANK[s]] = readers[s]
+    count = {"h4": 4, "f3": 3, "o0": 2, "o3": 3}
+    count.update({s: 16 for s in ("lh", "la", "lb", "lw", "lx", "dc", "ds")})
+
+    def wait(q, seen, needs):
+        for w in needs:
+            if w not in seen:
+                seen.add(w)
+                if w in far:
+                    q.wait_ge(S[w], far[w])
+                else:
+                    q.wait_ge(S[w + "_"], count.get(w, 1))
+
+    for q, order, done in ((y, SYNC, "st"), (t, TENSOR, None), (a, SCALAR, "st2"), (v, VECTOR, None)):
+        seen, stored = set(), 0
+        for s in order:
+            needs, calls = step[s]
+            wait(q, seen, needs)
+            for call in calls(q):
+                if s[0] == "y" or s == "bk":
+                    call.then_inc(S[done], 16)
+                    stored += 16
+                else:
+                    call.then_inc(S[s + "_"], 16 if count.get(s) == 16 else 1)
+        if stored:
+            q.wait_ge(S[done], stored)
+
+    far8 = 8 * SET
+    for h in range(2):
+        g.iota(T.k0[:, GRP * h:GRP * (h + 1)], [[far8, 8], [16 * h - 8, 2]], -8 * h, -far8 // BLK,
+               allow_small_or_imprecise_dtypes=True).then_inc(S.parts, 1)
+    g.iota(T.k2[:, :], [[8 * NBIT, NR], [8 * far8, 2]], 8 * (NBIT - 1), 0,
+           allow_small_or_imprecise_dtypes=True).then_inc(S.parts, 1)
+
+    sent, seen = [0], set()
 
     def send(*moves):
         tr = []
         for dst, eng, sem, src, out in moves:
-            a = topo.addr(dst)
-            tr.append(RemoteDMATransfer(dst_ids=[DstId(rid=a[0], pnc=a[1])], dma_engine_mask=_bits(eng),
+            ad_ = topo.addr(dst)
+            tr.append(RemoteDMATransfer(dst_ids=[DstId(rid=ad_[0], pnc=ad_[1])], dma_engine_mask=_bits(eng),
                                         remote_sem=S[sem], srcs=[src], dsts=[out]))
             sent[0] += len(eng)
         g.remote_dma_fused(tr, local_sem=S.sent)
 
-    y = g.sync
-    y.dma_start(T.eb[:, 0:4 * HALF], T.e[:, 0:4 * HALF]).then_inc(S.l_e0, 16)
-    y.dma_start(T.eb[:, 4 * HALF:], T.e[:, 4 * HALF:]).then_inc(S.l_e1, 16)
-    y.dma_start(T.wb[:, :], T.qw[:, :]).then_inc(S.l_w, 16)
-    a = g.scalar
-    a.dma_start(T.hb[:, 0:4 * HPC], T.hp[:, 0:4 * HPC]).then_inc(S.l_hp, 16)
-    a.dma_start(T.xb[:, :], T.x[:, :]).then_inc(S.l_x, 16)
-    nz = OWN - ZFROM
-    y.wait_ge(S.q_z, 1)
-    y.dma_start(cd("HC", ZFROM, OWN), cd("HC", 0, nz)).then_inc(S.zc, 16)
-    y.dma_start(pl("HS", ZFROM, OWN), pl("HS", 0, nz)).then_inc(S.zc, 16)
+    def piece(p, k):
+        return pl("ES%d" % k, 0, KCOL) if p == "s" else cd("EC%d" % k, *{"a": (0, HALF), "b": (HALF, KCOL)}[p])
 
-    slots = [(nb, on, 0), (mate, off[:oh], 1), (diag, off[oh:], 2)]
-    g.wait_ge(S.q_hp, 1)
+    slots = [(nb, on[:oh], 0), (mate, off[:oh], 1), (diag, off[oh:], 2)]
+    wait(g, seen, ["qh"])
     for view, src, name in ((cd, "HQ", "HC"), (pl, "HQS", "HS")):
-        send(*[(d, en, "hpin", view(src, 0, SLOT), view(name, LAND + SLOT * k, LAND + SLOT * (k + 1)))
+        send(*[(d, en, "planes", view(src, 0, NBIT), view(name, LAND + NBIT * k, LAND + NBIT * (k + 1)))
                for d, en, k in slots])
-    g.wait_ge(S.q_e0, 1)
-    send((mate, off, "m0", cd("EC0", 0, HALF), cd("EC2", 0, HALF)), (nb, on, "nbin", cd("EC0", 0, HALF), cd("EC1", 0, HALF)))
-    g.wait_ge(S.q_e1, 1)
-    send((mate, off, "m1", cd("EC0", HALF, KCOL), cd("EC2", HALF, KCOL)),
-         (nb, on, "nbin", cd("EC0", HALF, KCOL), cd("EC1", HALF, KCOL)))
-    send((mate, off, "m1", pl("ES0", 0, KCOL), pl("ES2", 0, KCOL)), (nb, on, "nbin", pl("ES0", 0, KCOL), pl("ES1", 0, KCOL)))
-    send((diag, off, "d1", cd("EC0", HALF, KCOL), cd("EC3", HALF, KCOL)))
-    send((diag, off, "d1", pl("ES0", 0, KCOL), pl("ES3", 0, KCOL)))
-    g.wait_ge(S.m0, len(off))
-    send((nb, on, "d0", cd("EC2", 0, HALF), cd("EC3", 0, HALF)))
+    ways = {"n": (nb, on, 0, 1), "m": (mate, off, 0, 2), "d": (diag, off, 0, 3), "r": (nb, on, 2, 3)}
+    for call in CALLS:
+        for p, w in call:
+            wait(g, seen, [p + "2"] if w == "r" else {"a": ["qa"], "b": ["qb"], "s": ["qa", "qb"]}[p])
+        send(*[(ways[w][0], ways[w][1], p + str(ways[w][3]), piece(p, ways[w][2]), piece(p, ways[w][3])) for p, w in call])
     g.wait_ge(S.sent, sent[0])
-
-    t = g.tensor
-
-    def planes(bank, moves, sem):
-        for i, (f, x0, n) in enumerate(moves):
-            m = t.matmul_mx(T[bank][:, 0:n], T.HC[:, f:f + 128], T.HS[:, f:f + 128], T.XC[:, x0:x0 + n], T.XS[:, x0:x0 + n],
-                            i == 0, i == len(moves) - 1)
-        m.then_inc(S[sem], 1)
-
-    def tables(k, banks):
-        for o in range(OUT):
-            w = slice(128 * o, 128 * o + 128)
-            t.matmul_mx(T[banks[o]][:, 0:KCOL], T.WC[:, w], T.WS[:, w], T["EC%d" % k][:, 0:KCOL], T["ES%d" % k][:, 0:KCOL],
-                        True, True).then_inc(S["t%d%d" % (k, o)], 1)
-
-    t.wait_ge(S.q_h4, 1)
-    t.wait_ge(S.q_x, 1)
-    t.wait_ge(S.q_z, 1)
-    t.wait_ge(S.zc, 32)
-    planes("p0", [(OWN - SLOT * s, SUB * s, SUB) for s in range(3)], "t_o")
-    t.wait_ge(S.q_e0, 1)
-    t.wait_ge(S.q_e1, 1)
-    t.wait_ge(S.q_w, 1)
-    tables(0, ("p2", "p3"))
-    t.wait_ge(S.hpin, 2 * (len(on) + 2 * oh))
-    for h in range(2):
-        planes(("p1", "p4")[h], [(LAND - BLK * b, PART * h, PART) for b in range(4)], "t_r%d" % h)
-    t.wait_ge(S.nbin, 3 * len(on))
-    tables(1, ("p5", "p6"))
-    t.wait_ge(S.m0, len(off))
-    t.wait_ge(S.m1, 2 * len(off))
-    t.wait_ge(S.bit0, 2)
-    tables(2, ("p7", "p0"))
-    t.wait_ge(S.c00, 1)
-    t.wait_ge(S.c01, 1)
-    t.wait_ge(S.d1, 2 * len(off))
-    t.wait_ge(S.d0, len(on))
-    tables(3, ("p2", "p3"))
-    bank = {(0, 0): "p2", (0, 1): "p3", (1, 0): "p5", (1, 1): "p6", (2, 0): "p7", (2, 1): "p0", (3, 0): "p2", (3, 1): "p3"}
-
-    def col(k, o):
-        c = (ranks[k] * OUT + o) * TOK
-        return slice(c, c + TOK)
-
-    def lst(k):
-        return T.offo[:, 0:RUNS] if k == 0 else T.offr[:, RUNS * (k - 1):RUNS * k]
-
-    def pick(k, o):
-        return T["G%d%d" % (k, o)][:, 0:KCOL].indirect(lst(k))
-
-    def list_made(q, k):
-        q.wait_ge(S["off%d" % k], 3 if k == 0 else 1)
-
-    v = g.vector
-    gt, mu, ad = AluOpType.is_gt, AluOpType.mult, AluOpType.add
-
-    def vcopy(k, o):
-        v.wait_ge(S["t%d%d" % (k, o)], 1)
-        v.tensor_copy(T["G%d%d" % (k, o)][:, 0:KCOL], T[bank[k, o]][:, 0:KCOL]).then_inc(S["c%d%d" % (k, o)], 1)
-
-    def vpick(k, o):
-        list_made(v, k)
-        v.wait_ge(S["c%d%d" % (k, o)], 1)
-        v.tensor_copy(T.yst[:, col(k, o)], pick(k, o)).then_inc(S["y%d%d" % (k, o)], 1)
-
-    def turn(p, n, sem, bt, r0, sb, tr, st):
-        r1 = r0 + n // 16
-        v.wait_ge(S[sem], 1)
-        for h in range(2):
-            v.tensor_scalar(bt[:, r0:r1, 16 * h:16 * h + 16], T[p][:, 0:n], 0.0, None, gt).then_inc(S[sb], 1)
-        v.wait_ge(S[sb], 2)
-        v.transpose(tr[:, BLK * r0:BLK * r1], bt[:, r0:r1, :]).then_inc(S[st], 1)
-
-    v.memset(T.h4[:, :], 0.0).then_inc(S.k_z, 1)
-    v.memset(T.hb[:, 4 * HPC:], 0.0).then_inc(S.k_h, 1)
-    v.wait_ge(S.k_z, 1)
-    v.quantize_mx(T.HC[:, 0:LAND], T.HS[:, 0:LAND], T.h4[:, 0:4 * LAND]).then_inc(S.q_z, 1)
-    v.memset(T.mul[:, :], 0.5).then_inc(S.k_a, 1)
-    v.wait_ge(S.k_a, 1)
-    for k in range(3):
-        v.memset(T.mul[:, SLOT * k:FREE:BLK], 0.0).then_inc(S.k_mul, 1)
-    v.memset(T.bf[0:BLK, :, :], 0.0).then_inc(S.k_bf, 1)
-    v.wait_ge(S.l_hp, 16)
-    v.wait_ge(S.k_h, 1)
-    v.quantize_mx(T.HQ[:, :], T.HQS[:, :], T.hb[:, :]).then_inc(S.q_hp, 1)
-    for h in range(2):
-        c = slice(HALF * h, HALF * h + HALF)
-        v.wait_ge(S["l_e%d" % h], 16)
-        v.quantize_mx(T.EC0[:, c], T.ES0[:, c], T.eb[:, 4 * HALF * h:4 * HALF * (h + 1)]).then_inc(S["q_e%d" % h], 1)
-        if h == 0:
-            v.wait_ge(S.h4c, 4)
-            v.quantize_mx(T.HC[:, OWN:], T.HS[:, OWN:], T.h4[:, 4 * LAND:]).then_inc(S.q_h4, 1)
-    v.wait_ge(S.l_x, 16)
-    v.quantize_mx(T.XC[:, :], T.XS[:, :], T.xb[:, :]).then_inc(S.q_x, 1)
-    v.wait_ge(S.l_w, 16)
-    v.quantize_mx(T.WC[:, :], T.WS[:, :], T.wb[:, :]).then_inc(S.q_w, 1)
-    v.wait_ge(S.k_mul, 3)
-    turn("p0", SUB, "t_o", T.bits0, 0, "bit0", T.tr0, "trn0")
-    v.wait_ge(S.trn0, 1)
-    v.tensor_tensor_scan(T.sc0[:, :], T.mul[:, 0:2 * SUB], T.tr0[:, :], 0.0, mu, ad).then_inc(S.scn0, 1)
-    v.wait_ge(S.scn0, 1)
-    q8 = SUB // 16
-    for s in range(3):
-        v.tensor_scalar(T.offo[:, q8 * s:q8 * (s + 1)], T.sc0[:, SLOT * s + NBIT - 1:2 * SUB:BLK], 256.0, None,
-                        mu).then_inc(S.off0, 1)
-    for h in range(2):
-        turn(("p1", "p4")[h], PART, "t_r%d" % h, T.bits1, RUNS // 2 * h, "bit%d" % (1 + h), T.tr1, "trn1")
-    v.wait_ge(S.trn1, 2)
-    v.tensor_tensor_scan(T.sc1[:, :], T.mul[:, :], T.tr1[:, :], 0.0, mu, ad).then_inc(S.scn1, 1)
-    v.wait_ge(S.scn1, 1)
-    for k in range(3):
-        v.tensor_scalar(T.offr[:, RUNS * k:RUNS * (k + 1)], T.sc1[:, SLOT * k + NBIT - 1:FREE:BLK], 256.0, None,
-                        mu).then_inc(S["off%d" % (k + 1)], 1)
-    vpick(1, 0)
-    v.wait_ge(S.k_bf, 1)
-    for k in (0, 2, 3):
-        list_made(v, k)
-    v.tensor_copy(T.bf[0:BLK, 0, 0:RUNS], T.offo[0:BLK, :]).then_inc(S.bfc, 1)
-    v.tensor_copy(T.bf[0:BLK, 1:4, 0:RUNS], T.offr[0:BLK, :]).then_inc(S.bfc, 1)
-    v.wait_ge(S.bfc, 2)
-    v.transpose(T.tb[0:BLK, :, :], T.bf[0:BLK, :, :]).then_inc(S.v_tb, 1)
-    vpick(2, 0)
-    vcopy(3, 0)
-    vpick(3, 0)
-
-    def acopy(k, o):
-        a.wait_ge(S["t%d%d" % (k, o)], 1)
-        a.activation(T["G%d%d" % (k, o)][:, 0:KCOL], T[bank[k, o]][:, 0:KCOL], cp).then_inc(S["c%d%d" % (k, o)], 1)
-
-    def apick(k, o):
-        list_made(a, k)
-        a.wait_ge(S["c%d%d" % (k, o)], 1)
-        a.activation(T.yst[:, col(k, o)], pick(k, o), cp).then_inc(S["y%d%d" % (k, o)], 1)
-
-    a.wait_ge(S.l_hp, 16)
-    a.wait_ge(S.k_z, 1)
-    for b in range(4):
-        f = 4 * (LAND + BLK * b)
-        a.activation(T.h4[:, f:f + 4 * HPC], T.hb[:, 0:4 * HPC], cp).then_inc(S.h4c, 1)
-    acopy(0, 0)
-    acopy(0, 1)
-    apick(0, 0)
-    apick(0, 1)
-    acopy(1, 0)
-    acopy(1, 1)
-    acopy(2, 0)
-    acopy(2, 1)
-    apick(1, 1)
-    apick(2, 1)
-    acopy(3, 1)
-    apick(3, 1)
-    a.wait_ge(S.y31, 1)
-    a.dma_start(T.y[:, col(3, 1)], T.yst[:, col(3, 1)]).then_inc(S.st2, 16)
-    a.wait_ge(S.st2, 16)
-
-    n = [0]
-
-    def store(k, o):
-        y.wait_ge(S["y%d%d" % (k, o)], 1)
-        y.dma_start(T.y[:, col(k, o)], T.yst[:, col(k, o)]).then_inc(S.st, 16)
-        n[0] += 16
-
-    for k, o in ((0, 0), (0, 1), (1, 0), (1, 1)):
-        store(k, o)
-    y.wait_ge(S.v_tb, 1)
-    for k in range(4):
-        y.dma_start(T.bk[ranks[k]:ranks[k] + 1, :], T.tb[0:RUNS, k, 0:16]).then_inc(S.st, 16)
-        n[0] += 16
-    for k, o in ((2, 0), (2, 1), (3, 0)):
-        store(k, o)
-    y.wait_ge(S.st, n[0])

@@ -6,22 +6,24 @@ BLK = 32
 GRP = 16
 CH = TOK // BLK
 RUNS = TOK // GRP
-SET = NR * NBIT
-PER = 3
+SLOT = NBIT + 1
+SET = 3 * SLOT
+PER = 4
 BANKS = CH // PER
 HPC = 16
+LEAD = 8
 LAND = 128
-OWN = LAND + 3 * NBIT
-TAIL = LAND + 48
+TAIL = LAND + BLK
 OWN4 = TAIL + 128
-SLOT = 10
+FINE = 16
+TINY = 1e-37
 SUB = TOK // 3
 HALF = KCOL // 2
-SCW = 2 * BLK * NBIT
+SCW = 2 * BLK * SLOT
 
 _X4 = "float8_e4m3fn_x4"
 SCRATCH = {
-    "hb": ("sbuf", [128, 4 * HPC + 512], "bfloat16"), "h4": ("sbuf", [128, 512], "bfloat16"),
+    "hb": ("sbuf", [128, LEAD + 4 * HPC + 512], "bfloat16"), "h4": ("sbuf", [128, 512], "bfloat16"),
     "HQ": ("sbuf", [128, 128], _X4), "HQS": ("sbuf", [128, 128], "uint8"),
     "xb": ("sbuf", [128, 4 * TOK], "bfloat16"),
     "wb": ("sbuf", [128, 4 * 128 * OUT], "bfloat16"),
@@ -30,14 +32,15 @@ SCRATCH = {
     "XC": ("sbuf", [128, TOK + 128], _X4), "XS": ("sbuf", [128, TOK + 128], "uint8"),
     "WC": ("sbuf", [128, 128 * OUT], _X4), "WS": ("sbuf", [128, 128 * OUT], "uint8"),
     "mul": ("sbuf", [128, PER * SET], "bfloat16"), "bits": ("sbuf", [128, CH * SET], "bfloat16"),
-    "sc": ("sbuf", [128, SCW], "float32"), "turn": ("sbuf", [128, 2, 2, GRP], "float32"),
+    "sc": ("sbuf", [128, SCW], "bfloat16"), "turn": ("sbuf", [128, 2, 2, GRP], "bfloat16"),
+    "bkf": ("sbuf", [128, 2, BLK], "float32"), "ob": ("sbuf", [128, BLK], "float32"), "obt": ("sbuf", [128, BLK], "float32"),
     "mul0": ("sbuf", [128, 2 * SUB], "bfloat16"), "bits0": ("sbuf", [128, SUB // GRP, BLK], "bfloat16"),
     "tr0": ("sbuf", [128, 2 * SUB], "bfloat16"), "sc0": ("sbuf", [128, 2 * SUB], "float16"),
     "list0": ("sbuf", [128, RUNS], "uint16"),
     "k0": ("sbuf", [128, BLK], "float32"), "k1": ("sbuf", [128, BLK], "float32"),
-    "k2": ("sbuf", [128, 8], "float32"), "k3": ("sbuf", [128, 8], "float32"), "k4": ("sbuf", [128, 8], "float32"),
-    "k5": ("sbuf", [128, 8], "float32"), "order": ("sbuf", [128, 8], "uint16"),
-    "lists": ("sbuf", [128, NR * BLK], "uint16"),
+    "k2": ("sbuf", [128, 6], "float32"), "k3": ("sbuf", [128, 6], "float32"), "k4": ("sbuf", [128, 6], "float32"),
+    "k5": ("sbuf", [128, 6], "float32"), "order": ("sbuf", [128, 6], "uint16"),
+    "lists": ("sbuf", [128, 3 * BLK], "uint16"),
     "yst": ("sbuf", [128, NR * OUT * TOK], "float32"),
 }
 for _k in range(NR):
@@ -48,20 +51,23 @@ for _k in range(NR):
 for _k in range(8):
     SCRATCH["p%d" % _k] = ("psum", [128, 512], "float32")
 
-CALLS = [["am", "an"], ["sm", "sn"], ["bm", "bn"], ["bd"], ["ar"], ["sr"]]
-SYNC = ["lh", "lx", "la", "lb", "lw", "y00", "y01", "bk", "y11", "y10", "y20", "y21", "y31"]
-TENSOR = ["mo", "m00", "m01", "mb0", "mb1", "mb2", "mb3", "m10a", "m11a", "m10b", "m11b", "m20a", "m21a", "m20b", "m21b",
-          "m30", "m31"]
-SCALAR = ["f0", "f1", "f2", "f3", "h4", "dc", "ds", "c00", "c01", "p00", "p01", "c10a", "c11a", "c20a", "c21a", "c21b",
-          "p11", "c30", "p21", "p30", "y30"]
-VECTOR = ["zh", "z0", "k1", "zs", "k2", "z1", "k3", "qh", "k4", "qx", "k5", "q4", "qa", "qb", "qw", "o0", "qy", "o1", "o2",
-          "o3", "g0", "g1", "u0", "g2", "u1", "g3", "u2", "u3", "c10b", "t1", "c11b", "t2", "c20b", "ls", "p10", "p20",
-          "c31", "p31"]
-BANK = {"mo": 7, "mb0": 4, "mb1": 5, "mb2": 6, "mb3": 7, "m00": 0, "m01": 1, "m10a": 2, "m11a": 3, "m10b": 4, "m11b": 5,
-        "m20a": 0, "m21a": 1, "m20b": 6, "m21b": 7, "m30": 2, "m31": 3}
+CALLS = ["planes", ["am", "an"], ["sm", "sn"], ["bm", "bn"], ["bd"], ["ar"], ["sr"]]
+SYNC = ["lh", "lx", "la", "lw", "lb", "y0", "ybo", "yb1", "yb2", "yb3", "y1", "y20", "y21", "y30", "y31"]
+TENSOR = ["mo", "m00a", "m01a", "m00b", "m01b", "mb0", "mb1", "mb2", "m10a", "m11a", "m10b", "m11b", "m20a", "m21a",
+          "m20b", "m21b", "m30", "m31"]
+SCALAR = ["f0", "f1", "dc", "ds", "k2", "h4", "k3", "f2", "k4", "f3", "o0", "c00a", "c01a", "c00b", "c01b", "p01", "p00a", "c10a", "c11a", "c11b",
+          "bf", "c21a", "c20b", "p10", "p21e", "c30", "p21f", "p30d", "p31b"]
+VECTOR = ["zh", "zs", "z0", "zb", "k1", "qh", "z1", "qx", "q4", "qa", "qw", "qb", "o1", "qy", "o2", "k5",
+          "o3", "p00b", "g0", "g1", "u0", "g2", "u1", "o4", "u2", "o5", "t1", "c10b", "t2", "c20a", "l1",
+          "l2", "c21b", "p11", "p20", "c31", "p30c", "p31a"]
+BANK = {"mo": 7, "mb0": 4, "mb1": 5, "mb2": 6, "m00a": 0, "m01a": 1, "m00b": 2, "m01b": 3, "m10a": 7, "m11a": 3,
+        "m10b": 4, "m11b": 5, "m20a": 0, "m21a": 1, "m20b": 6, "m21b": 2, "m30": 7, "m31": 3}
+RUN = {"": (0, RUNS), "a": (0, RUNS // 2), "b": (RUNS // 2, RUNS), "c": (0, 10), "d": (10, RUNS),
+       "e": (0, 16), "f": (16, RUNS)}
+HOLD = {"y0": ["b2"]}
 
 SEMAPHORES = (["sent", "planes", "parts", "st", "st2"] + [p + w for p in "abs" for w in "123"]
-              + [s + "_" for s in SYNC + TENSOR + SCALAR + VECTOR if s[0] != "y" and s != "bk"])
+              + [s + "_" for s in SYNC + TENSOR + SCALAR + VECTOR if s[0] != "y"])
 
 
 def _bits(engines):
@@ -73,8 +79,8 @@ def rank_program(g, core, T, topo):
     if rank is None:
         return
     S = T.sem
-    cp, ident = ActivationFunctionType.Copy, ActivationFunctionType.Identity
-    gt, lt, mu, ad = AluOpType.is_gt, AluOpType.is_lt, AluOpType.mult, AluOpType.add
+    cp, ident, sign = ActivationFunctionType.Copy, ActivationFunctionType.Identity, ActivationFunctionType.Sign
+    gt, mu, ad, sub = AluOpType.is_gt, AluOpType.mult, AluOpType.add, AluOpType.subtract
     nb = mate = diag = None
     for c in T.cores:
         if c == core:
@@ -89,10 +95,10 @@ def rank_program(g, core, T, topo):
     on = [e for e in topo.engines(core, nb) if e not in off]
     oh = len(off) // 2
     ranks = [rank, T.rank_of(nb), T.rank_of(mate), T.rank_of(diag)]
-    slot = [3, 0, 1, 2]
     y, a, v, t = g.sync, g.scalar, g.vector, g.tensor
-    zero = 4 * HPC
+    zero = LEAD + 4 * HPC
     n3 = PER * SET
+    wide = FINE * SET
 
     def cd(name, c0, c1):
         return T[name][:, c0:c1].bitcast(dt.uint8)
@@ -101,7 +107,7 @@ def rank_program(g, core, T, topo):
         return T[name][:, c0:c1]
 
     step = {}
-    far = {"planes": 2 * 3 * oh, "parts": 3}
+    far = {"planes": 5 * oh + oh // 2, "parts": 3}
     far.update({p + k: len(off) for p in "abs" for k in "123"})
 
     def load(out, src):
@@ -122,73 +128,91 @@ def rank_program(g, core, T, topo):
         return calls
 
     H, X, W = ("HC", "HS"), ("XC", "XS"), ("WC", "WS")
-    step["lh"] = load(T.hb[:, 0:zero], T.hp[:, 0:zero])
+    step["lh"] = load(T.hb[:, LEAD:zero], T.hp[:, 0:4 * HPC])
     step["la"] = load(T.eb[:, 0:4 * HALF], T.e[:, 0:4 * HALF])
     step["lb"] = load(T.eb[:, 4 * HALF:], T.e[:, 4 * HALF:])
     step["lw"] = load(T.wb[:, :], T.qw[:, :])
     step["lx"] = load(T.xb[:, :], T.x[:, :])
-    step["zh"] = [], lambda q: [q.memset(T.hb[:, zero:], 0.0)]
+    step["zh"] = [], lambda q: [q.memset(T.hb[:, zero:], 0.0), q.memset(T.hb[:, 0:LEAD], 0.0)]
     step["zs"] = [], lambda q: [q.memset(T.sc[:, CH * SET:], 0.0)]
     step["z0"] = quantise(["zh"], "HC", "HS", 0, LAND, T.hb[:, zero:])
     step["z1"] = quantise(["zh"], "HC", "HS", TAIL, OWN4, T.hb[:, zero:])
-    step["qh"] = quantise(["zh", "lh"], "HQ", "HQS", 0, 128, T.hb[:, 0:512])
+    step["qh"] = quantise(["zh", "lh"], "HQ", "HQS", 0, 128, T.hb[:, LEAD - 4:LEAD + 508])
     step["qa"] = quantise(["la"], "EC0", "ES0", 0, HALF, T.eb[:, 0:4 * HALF])
     step["qb"] = quantise(["lb"], "EC0", "ES0", HALF, KCOL, T.eb[:, 4 * HALF:])
     step["qw"] = quantise(["lw"], "WC", "WS", 0, 128 * OUT, T.wb[:, :])
     step["qx"] = quantise(["lx"], "XC", "XS", 0, TOK, T.xb[:, :])
     step["qy"] = quantise(["lx"], "XC", "XS", TOK, TOK + 128, T.xb[:, 0:512])
     step["q4"] = quantise(["h4"], "HC", "HS", OWN4, OWN4 + 128, T.h4[:, :])
-    step["h4"] = ["zh", "lh"], lambda q: [move(q, T.h4[:, 4 * BLK * b:4 * BLK * (b + 1)], T.hb[:, 0:4 * BLK]) for b in range(4)]
-    step["dc"] = ["qh"], lambda q: [q.dma_start(cd("HC", OWN, TAIL), cd("HQ", 0, TAIL - OWN))]
-    step["ds"] = ["qh"], lambda q: [q.dma_start(pl("HS", OWN, TAIL), pl("HQS", 0, TAIL - OWN))]
+    step["h4"] = ["zh", "lh"], lambda q: [move(q, T.h4[:, 4 * BLK * b:4 * BLK * (b + 1)], T.hb[:, LEAD:LEAD + 4 * BLK])
+                                          for b in range(4)]
+    step["dc"] = ["z0"], lambda q: [q.dma_start(cd("HC", LAND + SET, TAIL), cd("HC", 0, BLK - SET))]
+    step["ds"] = ["z0"], lambda q: [q.dma_start(pl("HS", LAND + SET, TAIL), pl("HS", 0, BLK - SET))]
     step["f0"] = ["zh"], lambda q: [q.activation(T.mul[:, :], T.hb[:, zero:zero + n3], ident, bias=0.5)]
     step["f1"] = ["zh"], lambda q: [q.activation(T.mul0[:, :], T.hb[:, zero:zero + 2 * SUB], ident, bias=0.5)]
-    step["f2"] = ["f0"], lambda q: [move(q, T.mul[:, 0::NBIT], T.hb[:, zero:zero + n3 // NBIT])]
+    step["f2"] = ["f0"], lambda q: [q.activation(T.mul[:, i::SLOT], T.hb[:, zero:zero + n3 // SLOT], ident, bias=float(i))
+                                    for i in range(2)]
     step["f3"] = ["f1"], lambda q: [move(q, T.mul0[:, SLOT * s::BLK], T.hb[:, zero:zero + 2 * SUB // BLK]) for s in range(3)]
     step["k1"] = ["parts"], lambda q: [q.transpose(T.k1[:, :], T.k0[:, :])]
-    step["k2"] = ["k1"], lambda q: [q.tensor_scalar(T.k3[:, :], T.k2[:, :], T.k1[:, 0:1], 0.125, ad, mu)]
-    step["k3"] = ["k2"], lambda q: [q.tensor_scalar(T.k4[:, :], T.k3[:, :], 0.0, float(CH * SET), lt, mu)]
-    step["k4"] = ["k3"], lambda q: [q.tensor_tensor(T.k5[:, :], T.k3[:, :], T.k4[:, :], ad)]
-    step["k5"] = ["k4"], lambda q: [q.tensor_copy(T.order[:, :], T.k5[:, :])]
+    mine = T.k1[:, 0:1]
+    step["k2"] = ["k1"], lambda q: [q.activation(T.k3[:, 0:1], mine, sign, bias=wide / 2.0)]
+    step["k3"] = ["k2"], lambda q: [q.activation(T.k4[:, 0:1], T.k3[:, 0:1], ident, bias=mine, scale=-CH * wide / 2.0)]
+    step["k4"] = ["k3"], lambda q: [q.activation(T.k5[:, i::2], T.k2[:, i::2], ident, bias=b)
+                                    for i, b in enumerate((T.k4[:, 0:1], mine))]
+    step["k5"] = ["k4"], lambda q: [q.tensor_scalar(T.order[:, :], T.k5[:, :], 1.0 / FINE, None, mu)]
     po = T["p%d" % BANK["mo"]]
     q8 = SUB // GRP
     step["mo"] = ["qx", "z1", "q4"], products(BANK["mo"], SUB, [(H, OWN4 - SLOT * s, X, SUB * s) for s in range(3)])
-    step["o0"] = ["mo"], lambda q: [q.tensor_scalar(T.bits0[:, :, GRP * h:GRP * (h + 1)], po[:, 0:SUB], 0.0, 256.0, gt, mu)
+    step["o0"] = ["mo"], lambda q: [q.activation(T.bits0[:, :, GRP * h:GRP * (h + 1)], po[:, 0:SUB], sign, bias=-TINY)
                                     for h in range(2)]
     step["o1"] = ["o0"], lambda q: [q.transpose(T.tr0[:, :], T.bits0[:, :, :])]
     step["o2"] = ["o1", "f3"], lambda q: [q.tensor_tensor_scan(T.sc0[:, :], T.mul0[:, :], T.tr0[:, :], 0.0, mu, ad)]
-    step["o3"] = ["o2"], lambda q: [q.tensor_copy(T.list0[:, q8 * s:q8 * (s + 1)], T.sc0[:, SLOT * s + NBIT - 1::BLK])
-                                    for s in range(3)]
+    step["o3"] = ["o2"], lambda q: [q.tensor_scalar(T.list0[:, q8 * s:q8 * (s + 1)], T.sc0[:, SLOT * s + NBIT - 1::BLK],
+                                                    KCOL / 4.0, (KCOL - 1) / 2.0, mu, ad) for s in range(3)]
     readers = {"mo": ["o0"]}
     for b in range(BANKS):
         c = slice(n3 * b, n3 * (b + 1))
         mb = "mb%d" % b
         step[mb] = (["qx", "qy", "z0", "z1", "dc", "ds", "planes"],
                     products(BANK[mb], 128, [(X, BLK * (PER * b + j), H, LAND - SET * j) for j in range(PER)]))
-        step["g%d" % b] = [mb], lambda q, c=c, mb=mb: [q.tensor_scalar(T.bits[:, c], T["p%d" % BANK[mb]][:, 0:n3], 0.0, 256.0, gt, mu)]
+        step["g%d" % b] = [mb], lambda q, c=c, mb=mb: [q.tensor_scalar(T.bits[:, c], T["p%d" % BANK[mb]][:, 0:n3], 0.0, 0.5, gt, sub)]
         step["u%d" % b] = ["g%d" % b, "f2"], lambda q, c=c: [q.tensor_tensor_scan(T.sc[:, c], T.mul[:, :], T.bits[:, c], 0.0, mu, ad)]
         readers[mb] = ["g%d" % b]
     step["t1"] = (["zs"] + ["u%d" % b for b in range(BANKS)],
-                  lambda q: [q.transpose(T.turn[:, :, :, :], T.sc[:, NBIT - 1::NBIT])])
-    step["t2"] = ["t1"], lambda q: [q.transpose(T.sc[:, NBIT - 2::NBIT], T.turn[:, :, ::-1, :])]
-    step["ls"] = ["t2", "k5"], lambda q: [q.tensor_copy(T.lists[:, :], T.sc[:, 0:SCW].indirect(T.order[:, :]))]
-    first = BLK // NR * BLK
-    step["bk"] = ["t1"], lambda q: [q.dma_start(T.bk[ranks[j]:ranks[j] + 1, c], T.turn[slot[j]:e:NR, h, :, :])
-                                    for j in range(NR)
-                                    for h, c, e in ((0, slice(0, first), BLK), (1, slice(first, TOK), NR * CH - BLK))]
+                  lambda q: [q.transpose(T.turn[:, :, :, :], T.sc[:, SLOT - 1::SLOT])])
+    step["t2"] = ["t1"], lambda q: [q.transpose(T.sc[:, SLOT - 2::SLOT], T.turn[:, :, ::-1, :])]
+    for s, k0, k1 in (("l1", 0, 1), ("l2", 1, 3)):
+        step[s] = ["t2", "k5"], lambda q, k0=k0, k1=k1: [q.tensor_scalar(
+            T.lists[:, BLK * k0:BLK * k1], T.sc[:, 0:SCW].indirect(T.order[:, 2 * k0:2 * k1]), 256.0, 256.0, mu, ad)]
+    step["bf"] = ["t1"], lambda q: [q.activation(T.bkf[0:BLK, :, :], T.turn[0:BLK, :, :, :], ident, bias=256.0, scale=256.0)]
+
+    for j in range(3):
+        n, r = len(range(j, BLK, 3)), ranks[j + 1]
+        step["yb%d" % (j + 1)] = ["bf"], lambda q, j=j, n=n, r=r: [
+            q.dma_start(T.bk[r:r + 1, 0:BLK * n], T.bkf[j:BLK:3, 0, :]),
+            q.dma_start(T.bk[r:r + 1, BLK * n:], T.bkf[3 * n + j - BLK:3 * CH - BLK:3, 1, :])]
+    step["zb"] = [], lambda q: [q.memset(T.ob[0:BLK, :], 0.0)]
+    step["o4"] = ["zb", "o3"], lambda q: [q.tensor_copy(T.ob[0:BLK, 0:RUNS], T.list0[0:BLK, :])]
+    step["o5"] = ["o4"], lambda q: [q.transpose(T.obt[0:BLK, :], T.ob[0:BLK, :])]
+    step["ybo"] = ["o5"], lambda q: [q.dma_start(T.bk[rank:rank + 1, :], T.obt[0:RUNS, 0:GRP])]
     names = SYNC + TENSOR + SCALAR + VECTOR
     part = {"": (0, 2), "a": (0, 1), "b": (1, 2)}
     for s in names:
         if s in step:
             continue
-        what, k, o, (h0, h1) = s[0], int(s[1]), int(s[2]), part[s[3:]]
+        if len(s) == 2:
+            both = slice(ranks[int(s[1])] * OUT * TOK, (ranks[int(s[1])] + 1) * OUT * TOK)
+            step[s] = ([r for r in names if r[:2] == "p" + s[1]],
+                       lambda q, both=both: [q.dma_start(T.y[:, both], T.yst[:, both])])
+            continue
+        what, k, o, (h0, h1), (r0, r1) = s[0], int(s[1]), int(s[2]), part.get(s[3:], (0, 2)), RUN[s[3:]]
         ko = s[1:3]
         G = T["G" + ko]
         c0 = (ranks[k] * OUT + o) * TOK
-        tok = slice(c0 + h0 * TOK // 2, c0 + h1 * TOK // 2)
+        tok = slice(c0 + GRP * r0, c0 + GRP * r1)
         if what == "m":
-            pieces = (s[3:] or "ab") + "s"
-            needs = ["qw"] + (["q" + p for p in pieces[:-1]] if k == 0 else [p + s[1] for p in pieces])
+            pieces = s[3:] or "ab"
+            needs = ["qw"] + (["q" + p for p in pieces] if k == 0 else [p + s[1] for p in pieces + "s"])
             step[s] = needs, products(BANK[s], HALF * (h1 - h0), [(W, 128 * o, ("EC" + s[1], "ES" + s[1]), HALF * h0)])
             readers[s] = [r for r in names if r.startswith("c" + s[1:])]
         elif what == "c":
@@ -200,19 +224,20 @@ def rank_program(g, core, T, topo):
             step[s] = ([m] + [other] * apart,
                        lambda q, G=G, src=src, h0=h0, h1=h1: [move(q, G[:, HALF * h0:HALF * h1], src)])
         elif what == "p":
-            own = k == 0 and "o3" in names
-            f = 0 if own else BLK * slot[k]
-            lst = (T.list0 if own else T.lists)[:, f + h0 * RUNS // 2:f + h1 * RUNS // 2]
-            step[s] = (["o3" if own else "ls"] + [r for r in names if r.startswith("c" + ko)],
+            f = BLK * max(k - 1, 0)
+            lst = (T.lists if k else T.list0)[:, f + r0:f + r1]
+            step[s] = ([("o3", "l1", "l2", "l2")[k]] + [r for r in names if r.startswith("c" + ko)],
                        lambda q, G=G, tok=tok, lst=lst: [move(q, T.yst[:, tok], G[:, 0:KCOL].indirect(lst))])
         else:
-            step[s] = ([r for r in names if r.startswith("p" + s[1:])],
+            step[s] = ([r for r in names if r[:3] == "p" + ko and RUN[r[3:]][0] < r1 and r0 < RUN[r[3:]][1]],
                        lambda q, tok=tok: [q.dma_start(T.y[:, tok], T.yst[:, tok])])
+    for s, needs in HOLD.items():
+        step[s][0].extend(needs)
     held = {}
     for s in TENSOR:
         step[s][0].extend(held.get(BANK[s], []))
         held[BANK[s]] = readers[s]
-    count = {"h4": 4, "f3": 3, "o0": 2, "o3": 3}
+    count = {"k4": 2, "zh": 2, "f2": 2, "h4": 4, "f3": 3, "o0": 2, "o3": 3}
     count.update({s: 16 for s in ("lh", "la", "lb", "lw", "lx", "dc", "ds")})
 
     def wait(q, seen, needs):
@@ -230,7 +255,7 @@ def rank_program(g, core, T, topo):
             needs, calls = step[s]
             wait(q, seen, needs)
             for call in calls(q):
-                if s[0] == "y" or s == "bk":
+                if s[0] == "y":
                     call.then_inc(S[done], 16)
                     stored += 16
                 else:
@@ -238,11 +263,10 @@ def rank_program(g, core, T, topo):
         if stored:
             q.wait_ge(S[done], stored)
 
-    far8 = 8 * SET
     for h in range(2):
-        g.iota(T.k0[:, GRP * h:GRP * (h + 1)], [[far8, 8], [16 * h - 8, 2]], -8 * h, -far8 // BLK,
+        g.iota(T.k0[:, GRP * h:GRP * (h + 1)], [[wide, 8], [FINE * (2 * h - 1), 2]], -FINE * h, -wide // BLK,
                allow_small_or_imprecise_dtypes=True).then_inc(S.parts, 1)
-    g.iota(T.k2[:, :], [[8 * NBIT, NR], [8 * far8, 2]], 8 * (NBIT - 1), 0,
+    g.iota(T.k2[:, :], [[FINE * SLOT, 3], [(8 - CH // 2) * wide, 2]], FINE * (SLOT - 1) + CH // 2 * wide, 0,
            allow_small_or_imprecise_dtypes=True).then_inc(S.parts, 1)
 
     sent, seen = [0], set()
@@ -250,8 +274,8 @@ def rank_program(g, core, T, topo):
     def send(*moves):
         tr = []
         for dst, eng, sem, src, out in moves:
-            ad_ = topo.addr(dst)
-            tr.append(RemoteDMATransfer(dst_ids=[DstId(rid=ad_[0], pnc=ad_[1])], dma_engine_mask=_bits(eng),
+            at = topo.addr(dst)
+            tr.append(RemoteDMATransfer(dst_ids=[DstId(rid=at[0], pnc=at[1])], dma_engine_mask=_bits(eng),
                                         remote_sem=S[sem], srcs=[src], dsts=[out]))
             sent[0] += len(eng)
         g.remote_dma_fused(tr, local_sem=S.sent)
@@ -259,13 +283,15 @@ def rank_program(g, core, T, topo):
     def piece(p, k):
         return pl("ES%d" % k, 0, KCOL) if p == "s" else cd("EC%d" % k, *{"a": (0, HALF), "b": (HALF, KCOL)}[p])
 
-    slots = [(nb, on[:oh], 0), (mate, off[:oh], 1), (diag, off[oh:], 2)]
-    wait(g, seen, ["qh"])
-    for view, src, name in ((cd, "HQ", "HC"), (pl, "HQS", "HS")):
-        send(*[(d, en, "planes", view(src, 0, NBIT), view(name, LAND + NBIT * k, LAND + NBIT * (k + 1)))
-               for d, en, k in slots])
     ways = {"n": (nb, on, 0, 1), "m": (mate, off, 0, 2), "d": (diag, off, 0, 3), "r": (nb, on, 2, 3)}
     for call in CALLS:
+        if call == "planes":
+            wait(g, seen, ["qh"])
+            for view, src, name, near in ((pl, "HQS", "HS", on[:oh // 2]), (cd, "HQ", "HC", on[oh:])):
+                slots = [(nb, near, 0), (mate, off[:oh], 1), (diag, off[oh:], 2)]
+                send(*[(d, en, "planes", view(src, 0, SLOT), view(name, LAND + SLOT * k, LAND + SLOT * (k + 1)))
+                       for d, en, k in slots])
+            continue
         for p, w in call:
             wait(g, seen, [p + "2"] if w == "r" else {"a": ["qa"], "b": ["qb"], "s": ["qa", "qb"]}[p])
         send(*[(ways[w][0], ways[w][1], p + str(ways[w][3]), piece(p, ways[w][2]), piece(p, ways[w][3])) for p, w in call])

from concourse.bass import DstId, RemoteDMATransfer
from concourse.mybir import dt, AluOpType, ActivationFunctionType

TOK, NBIT, KCOL, OUT, NR = 384, 9, 512, 2, 4
BLK = 32
GRP = 16
CH = TOK // BLK
RUNS = TOK // GRP
SLOT = NBIT + 1
SET = 3 * SLOT
PER = 4
BANKS = CH // PER
HPC = 16
LEAD = 8
LAND = 128
TAIL = LAND + BLK
OWN4 = TAIL + 128
FINE = 16
TINY = 1e-37
SUB = TOK // 3
HALF = KCOL // 2
SCW = 2 * BLK * SLOT

_X4 = "float8_e4m3fn_x4"
SCRATCH = {
    "hb": ("sbuf", [128, LEAD + 4 * HPC + 512], "bfloat16"), "h4": ("sbuf", [128, 512], "bfloat16"),
    "HQ": ("sbuf", [128, 128], _X4), "HQS": ("sbuf", [128, 128], "uint8"),
    "xb": ("sbuf", [128, 4 * TOK], "bfloat16"),
    "wb": ("sbuf", [128, 4 * 128 * OUT], "bfloat16"),
    "eb": ("sbuf", [128, 4 * KCOL], "bfloat16"),
    "HC": ("sbuf", [128, OWN4 + 128], _X4), "HS": ("sbuf", [128, OWN4 + 128], "uint8"),
    "XC": ("sbuf", [128, TOK + 128], _X4), "XS": ("sbuf", [128, TOK + 128], "uint8"),
    "WC": ("sbuf", [128, 128 * OUT], _X4), "WS": ("sbuf", [128, 128 * OUT], "uint8"),
    "mul": ("sbuf", [128, PER * SET], "bfloat16"), "bits": ("sbuf", [128, CH * SET], "bfloat16"),
    "sc": ("sbuf", [128, SCW], "bfloat16"), "turn": ("sbuf", [128, 2, 2, GRP], "bfloat16"),
    "bkf": ("sbuf", [128, 2, BLK], "float32"), "ob": ("sbuf", [128, BLK], "float32"), "obt": ("sbuf", [128, BLK], "float32"),
    "mul0": ("sbuf", [128, 2 * SUB], "bfloat16"), "bits0": ("sbuf", [128, SUB // GRP, BLK], "bfloat16"),
    "tr0": ("sbuf", [128, 2 * SUB], "bfloat16"), "sc0": ("sbuf", [128, 2 * SUB], "float16"),
    "list0": ("sbuf", [128, RUNS], "uint16"),
    "k0": ("sbuf", [128, BLK], "float32"), "k1": ("sbuf", [128, BLK], "float32"),
    "k2": ("sbuf", [128, 6], "float32"), "k3": ("sbuf", [128, 6], "float32"), "k4": ("sbuf", [128, 6], "float32"),
    "k5": ("sbuf", [128, 6], "float32"), "order": ("sbuf", [128, 6], "uint16"),
    "lists": ("sbuf", [128, 3 * BLK], "uint16"),
    "yst": ("sbuf", [128, NR * OUT * TOK], "float32"),
}
for _k in range(NR):
    SCRATCH["EC%d" % _k] = ("sbuf", [128, KCOL], _X4)
    SCRATCH["ES%d" % _k] = ("sbuf", [128, KCOL], "uint8")
    for _o in range(OUT):
        SCRATCH["G%d%d" % (_k, _o)] = ("sbuf", [128, KCOL], "float32")
for _k in range(8):
    SCRATCH["p%d" % _k] = ("psum", [128, 512], "float32")

CALLS = ["planes", ["am", "an"], ["sm", "sn"], ["bm", "bn"], ["bd"], ["ar"], ["sr"]]
SYNC = ["lh", "lx", "la", "lw", "lb", "y0", "ybo", "yb1", "yb2", "yb3", "y1", "y20", "y21", "y30", "y31"]
TENSOR = ["mo", "m00a", "m01a", "m00b", "m01b", "mb0", "mb1", "mb2", "m10a", "m11a", "m10b", "m11b", "m20a", "m21a",
          "m20b", "m21b", "m30", "m31"]
SCALAR = ["f0", "f1", "dc", "ds", "k2", "h4", "k3", "f2", "k4", "f3", "o0", "c00a", "c01a", "c00b", "c01b", "p01", "p00a", "c10a", "c11a", "c11b",
          "bf", "c21a", "c20b", "p10", "p21e", "c30", "p21f", "p30d", "p31b"]
VECTOR = ["zh", "zs", "z0", "zb", "k1", "qh", "z1", "qx", "q4", "qa", "qw", "qb", "o1", "qy", "o2", "k5",
          "o3", "p00b", "g0", "g1", "u0", "g2", "u1", "o4", "u2", "o5", "t1", "c10b", "t2", "c20a", "l1",
          "l2", "c21b", "p11", "p20", "c31", "p30c", "p31a"]
BANK = {"mo": 7, "mb0": 4, "mb1": 5, "mb2": 6, "m00a": 0, "m01a": 1, "m00b": 2, "m01b": 3, "m10a": 7, "m11a": 3,
        "m10b": 4, "m11b": 5, "m20a": 0, "m21a": 1, "m20b": 6, "m21b": 2, "m30": 7, "m31": 3}
RUN = {"": (0, RUNS), "a": (0, RUNS // 2), "b": (RUNS // 2, RUNS), "c": (0, 10), "d": (10, RUNS),
       "e": (0, 16), "f": (16, RUNS)}
HOLD = {"y0": ["b2"]}

SEMAPHORES = (["sent", "planes", "parts", "st", "st2"] + [p + w for p in "abs" for w in "123"]
              + [s + "_" for s in SYNC + TENSOR + SCALAR + VECTOR if s[0] != "y"])


def _bits(engines):
    return sum(1 << e for e in engines)


def rank_program(g, core, T, topo):
    rank = T.rank_of(core)
    if rank is None:
        return
    S = T.sem
    cp, ident, sign = ActivationFunctionType.Copy, ActivationFunctionType.Identity, ActivationFunctionType.Sign
    gt, mu, ad, sub = AluOpType.is_gt, AluOpType.mult, AluOpType.add, AluOpType.subtract
    nb = mate = diag = None
    for c in T.cores:
        if c == core:
            continue
        if topo.chip(c) == topo.chip(core):
            nb = c
        elif topo.die(c) == topo.die(core):
            mate = c
        else:
            diag = c
    off = topo.engines(core, mate)
    on = [e for e in topo.engines(core, nb) if e not in off]
    oh = len(off) // 2
    ranks = [rank, T.rank_of(nb), T.rank_of(mate), T.rank_of(diag)]
    y, a, v, t = g.sync, g.scalar, g.vector, g.tensor
    zero = LEAD + 4 * HPC
    n3 = PER * SET
    wide = FINE * SET

    def cd(name, c0, c1):
        return T[name][:, c0:c1].bitcast(dt.uint8)

    def pl(name, c0, c1):
        return T[name][:, c0:c1]

    step = {}
    far = {"planes": 5 * oh + oh // 2, "parts": 3}
    far.update({p + k: len(off) for p in "abs" for k in "123"})

    def load(out, src):
        return [], lambda q: [q.dma_start(out, src)]

    def quantise(needs, c, s, c0, c1, src):
        return needs, lambda q: [q.quantize_mx(T[c][:, c0:c1], T[s][:, c0:c1], src)]

    def move(q, out, src):
        return q.tensor_copy(out, src) if q is v else q.activation(out, src, cp)

    def products(bank, n, views):
        def calls(q):
            for i, (w, f, m, h) in enumerate(views):
                last = q.matmul_mx(T["p%d" % bank][:, 0:n], T[w[0]][:, f:f + 128], T[w[1]][:, f:f + 128],
                                   T[m[0]][:, h:h + n], T[m[1]][:, h:h + n], i == 0, i == len(views) - 1)
            return [last]
        return calls

    H, X, W = ("HC", "HS"), ("XC", "XS"), ("WC", "WS")
    step["lh"] = load(T.hb[:, LEAD:zero], T.hp[:, 0:4 * HPC])
    step["la"] = load(T.eb[:, 0:4 * HALF], T.e[:, 0:4 * HALF])
    step["lb"] = load(T.eb[:, 4 * HALF:], T.e[:, 4 * HALF:])
    step["lw"] = load(T.wb[:, :], T.qw[:, :])
    step["lx"] = load(T.xb[:, :], T.x[:, :])
    step["zh"] = [], lambda q: [q.memset(T.hb[:, zero:], 0.0), q.memset(T.hb[:, 0:LEAD], 0.0)]
    step["zs"] = [], lambda q: [q.memset(T.sc[:, CH * SET:], 0.0)]
    step["z0"] = quantise(["zh"], "HC", "HS", 0, LAND, T.hb[:, zero:])
    step["z1"] = quantise(["zh"], "HC", "HS", TAIL, OWN4, T.hb[:, zero:])
    step["qh"] = quantise(["zh", "lh"], "HQ", "HQS", 0, 128, T.hb[:, LEAD - 4:LEAD + 508])
    step["qa"] = quantise(["la"], "EC0", "ES0", 0, HALF, T.eb[:, 0:4 * HALF])
    step["qb"] = quantise(["lb"], "EC0", "ES0", HALF, KCOL, T.eb[:, 4 * HALF:])
    step["qw"] = quantise(["lw"], "WC", "WS", 0, 128 * OUT, T.wb[:, :])
    step["qx"] = quantise(["lx"], "XC", "XS", 0, TOK, T.xb[:, :])
    step["qy"] = quantise(["lx"], "XC", "XS", TOK, TOK + 128, T.xb[:, 0:512])
    step["q4"] = quantise(["h4"], "HC", "HS", OWN4, OWN4 + 128, T.h4[:, :])
    step["h4"] = ["zh", "lh"], lambda q: [move(q, T.h4[:, 4 * BLK * b:4 * BLK * (b + 1)], T.hb[:, LEAD:LEAD + 4 * BLK])
                                          for b in range(4)]
    step["dc"] = ["z0"], lambda q: [q.dma_start(cd("HC", LAND + SET, TAIL), cd("HC", 0, BLK - SET))]
    step["ds"] = ["z0"], lambda q: [q.dma_start(pl("HS", LAND + SET, TAIL), pl("HS", 0, BLK - SET))]
    step["f0"] = ["zh"], lambda q: [q.activation(T.mul[:, :], T.hb[:, zero:zero + n3], ident, bias=0.5)]
    step["f1"] = ["zh"], lambda q: [q.activation(T.mul0[:, :], T.hb[:, zero:zero + 2 * SUB], ident, bias=0.5)]
    step["f2"] = ["f0"], lambda q: [q.activation(T.mul[:, i::SLOT], T.hb[:, zero:zero + n3 // SLOT], ident, bias=float(i))
                                    for i in range(2)]
    step["f3"] = ["f1"], lambda q: [move(q, T.mul0[:, SLOT * s::BLK], T.hb[:, zero:zero + 2 * SUB // BLK]) for s in range(3)]
    step["k1"] = ["parts"], lambda q: [q.transpose(T.k1[:, :], T.k0[:, :])]
    mine = T.k1[:, 0:1]
    step["k2"] = ["k1"], lambda q: [q.activation(T.k3[:, 0:1], mine, sign, bias=wide / 2.0)]
    step["k3"] = ["k2"], lambda q: [q.activation(T.k4[:, 0:1], T.k3[:, 0:1], ident, bias=mine, scale=-CH * wide / 2.0)]
    step["k4"] = ["k3"], lambda q: [q.activation(T.k5[:, i::2], T.k2[:, i::2], ident, bias=b)
                                    for i, b in enumerate((T.k4[:, 0:1], mine))]
    step["k5"] = ["k4"], lambda q: [q.tensor_scalar(T.order[:, :], T.k5[:, :], 1.0 / FINE, None, mu)]
    po = T["p%d" % BANK["mo"]]
    q8 = SUB // GRP
    step["mo"] = ["qx", "z1", "q4"], products(BANK["mo"], SUB, [(H, OWN4 - SLOT * s, X, SUB * s) for s in range(3)])
    step["o0"] = ["mo"], lambda q: [q.activation(T.bits0[:, :, GRP * h:GRP * (h + 1)], po[:, 0:SUB], sign, bias=-TINY)
                                    for h in range(2)]
    step["o1"] = ["o0"], lambda q: [q.transpose(T.tr0[:, :], T.bits0[:, :, :])]
    step["o2"] = ["o1", "f3"], lambda q: [q.tensor_tensor_scan(T.sc0[:, :], T.mul0[:, :], T.tr0[:, :], 0.0, mu, ad)]
    step["o3"] = ["o2"], lambda q: [q.tensor_scalar(T.list0[:, q8 * s:q8 * (s + 1)], T.sc0[:, SLOT * s + NBIT - 1::BLK],
                                                    KCOL / 4.0, (KCOL - 1) / 2.0, mu, ad) for s in range(3)]
    readers = {"mo": ["o0"]}
    for b in range(BANKS):
        c = slice(n3 * b, n3 * (b + 1))
        mb = "mb%d" % b
        step[mb] = (["qx", "qy", "z0", "z1", "dc", "ds", "planes"],
                    products(BANK[mb], 128, [(X, BLK * (PER * b + j), H, LAND - SET * j) for j in range(PER)]))
        step["g%d" % b] = [mb], lambda q, c=c, mb=mb: [q.tensor_scalar(T.bits[:, c], T["p%d" % BANK[mb]][:, 0:n3], 0.0, 0.5, gt, sub)]
        step["u%d" % b] = ["g%d" % b, "f2"], lambda q, c=c: [q.tensor_tensor_scan(T.sc[:, c], T.mul[:, :], T.bits[:, c], 0.0, mu, ad)]
        readers[mb] = ["g%d" % b]
    step["t1"] = (["zs"] + ["u%d" % b for b in range(BANKS)],
                  lambda q: [q.transpose(T.turn[:, :, :, :], T.sc[:, SLOT - 1::SLOT])])
    step["t2"] = ["t1"], lambda q: [q.transpose(T.sc[:, SLOT - 2::SLOT], T.turn[:, :, ::-1, :])]
    for s, k0, k1 in (("l1", 0, 1), ("l2", 1, 3)):
        step[s] = ["t2", "k5"], lambda q, k0=k0, k1=k1: [q.tensor_scalar(
            T.lists[:, BLK * k0:BLK * k1], T.sc[:, 0:SCW].indirect(T.order[:, 2 * k0:2 * k1]), 256.0, 256.0, mu, ad)]
    step["bf"] = ["t1"], lambda q: [q.activation(T.bkf[0:BLK, :, :], T.turn[0:BLK, :, :, :], ident, bias=256.0, scale=256.0)]

    for j in range(3):
        n, r = len(range(j, BLK, 3)), ranks[j + 1]
        step["yb%d" % (j + 1)] = ["bf"], lambda q, j=j, n=n, r=r: [
            q.dma_start(T.bk[r:r + 1, 0:BLK * n], T.bkf[j:BLK:3, 0, :]),
            q.dma_start(T.bk[r:r + 1, BLK * n:], T.bkf[3 * n + j - BLK:3 * CH - BLK:3, 1, :])]
    step["zb"] = [], lambda q: [q.memset(T.ob[0:BLK, :], 0.0)]
    step["o4"] = ["zb", "o3"], lambda q: [q.tensor_copy(T.ob[0:BLK, 0:RUNS], T.list0[0:BLK, :])]
    step["o5"] = ["o4"], lambda q: [q.transpose(T.obt[0:BLK, :], T.ob[0:BLK, :])]
    step["ybo"] = ["o5"], lambda q: [q.dma_start(T.bk[rank:rank + 1, :], T.obt[0:RUNS, 0:GRP])]
    names = SYNC + TENSOR + SCALAR + VECTOR
    part = {"": (0, 2), "a": (0, 1), "b": (1, 2)}
    for s in names:
        if s in step:
            continue
        if len(s) == 2:
            both = slice(ranks[int(s[1])] * OUT * TOK, (ranks[int(s[1])] + 1) * OUT * TOK)
            step[s] = ([r for r in names if r[:2] == "p" + s[1]],
                       lambda q, both=both: [q.dma_start(T.y[:, both], T.yst[:, both])])
            continue
        what, k, o, (h0, h1), (r0, r1) = s[0], int(s[1]), int(s[2]), part.get(s[3:], (0, 2)), RUN[s[3:]]
        ko = s[1:3]
        G = T["G" + ko]
        c0 = (ranks[k] * OUT + o) * TOK
        tok = slice(c0 + GRP * r0, c0 + GRP * r1)
        if what == "m":
            pieces = s[3:] or "ab"
            needs = ["qw"] + (["q" + p for p in pieces] if k == 0 else [p + s[1] for p in pieces + "s"])
            step[s] = needs, products(BANK[s], HALF * (h1 - h0), [(W, 128 * o, ("EC" + s[1], "ES" + s[1]), HALF * h0)])
            readers[s] = [r for r in names if r.startswith("c" + s[1:])]
        elif what == "c":
            m = "m" + s[1:] if "m" + s[1:] in BANK else "m" + ko
            f = HALF * h0 if m == "m" + ko else 0
            src = T["p%d" % BANK[m]][:, f:f + HALF * (h1 - h0)]
            other = "c" + ko + "a"
            apart = f and (other in VECTOR) != (s in VECTOR)
            step[s] = ([m] + [other] * apart,
                       lambda q, G=G, src=src, h0=h0, h1=h1: [move(q, G[:, HALF * h0:HALF * h1], src)])
        elif what == "p":
            f = BLK * max(k - 1, 0)
            lst = (T.lists if k else T.list0)[:, f + r0:f + r1]
            step[s] = ([("o3", "l1", "l2", "l2")[k]] + [r for r in names if r.startswith("c" + ko)],
                       lambda q, G=G, tok=tok, lst=lst: [move(q, T.yst[:, tok], G[:, 0:KCOL].indirect(lst))])
        else:
            step[s] = ([r for r in names if r[:3] == "p" + ko and RUN[r[3:]][0] < r1 and r0 < RUN[r[3:]][1]],
                       lambda q, tok=tok: [q.dma_start(T.y[:, tok], T.yst[:, tok])])
    for s, needs in HOLD.items():
        step[s][0].extend(needs)
    held = {}
    for s in TENSOR:
        step[s][0].extend(held.get(BANK[s], []))
        held[BANK[s]] = readers[s]
    count = {"k4": 2, "zh": 2, "f2": 2, "h4": 4, "f3": 3, "o0": 2, "o3": 3}
    count.update({s: 16 for s in ("lh", "la", "lb", "lw", "lx", "dc", "ds")})

    def wait(q, seen, needs):
        for w in needs:
            if w not in seen:
                seen.add(w)
                if w in far:
                    q.wait_ge(S[w], far[w])
                else:
                    q.wait_ge(S[w + "_"], count.get(w, 1))

    for q, order, done in ((y, SYNC, "st"), (t, TENSOR, None), (a, SCALAR, "st2"), (v, VECTOR, None)):
        seen, stored = set(), 0
        for s in order:
            needs, calls = step[s]
            wait(q, seen, needs)
            for call in calls(q):
                if s[0] == "y":
                    call.then_inc(S[done], 16)
                    stored += 16
                else:
                    call.then_inc(S[s + "_"], 16 if count.get(s) == 16 else 1)
        if stored:
            q.wait_ge(S[done], stored)

    for h in range(2):
        g.iota(T.k0[:, GRP * h:GRP * (h + 1)], [[wide, 8], [FINE * (2 * h - 1), 2]], -FINE * h, -wide // BLK,
               allow_small_or_imprecise_dtypes=True).then_inc(S.parts, 1)
    g.iota(T.k2[:, :], [[FINE * SLOT, 3], [(8 - CH // 2) * wide, 2]], FINE * (SLOT - 1) + CH // 2 * wide, 0,
           allow_small_or_imprecise_dtypes=True).then_inc(S.parts, 1)

    sent, seen = [0], set()

    def send(*moves):
        tr = []
        for dst, eng, sem, src, out in moves:
            at = topo.addr(dst)
            tr.append(RemoteDMATransfer(dst_ids=[DstId(rid=at[0], pnc=at[1])], dma_engine_mask=_bits(eng),
                                        remote_sem=S[sem], srcs=[src], dsts=[out]))
            sent[0] += len(eng)
        g.remote_dma_fused(tr, local_sem=S.sent)

    def piece(p, k):
        return pl("ES%d" % k, 0, KCOL) if p == "s" else cd("EC%d" % k, *{"a": (0, HALF), "b": (HALF, KCOL)}[p])

    ways = {"n": (nb, on, 0, 1), "m": (mate, off, 0, 2), "d": (diag, off, 0, 3), "r": (nb, on, 2, 3)}
    for call in CALLS:
        if call == "planes":
            wait(g, seen, ["qh"])
            for view, src, name, near in ((pl, "HQS", "HS", on[:oh // 2]), (cd, "HQ", "HC", on[oh:])):
                slots = [(nb, near, 0), (mate, off[:oh], 1), (diag, off[oh:], 2)]
                send(*[(d, en, "planes", view(src, 0, SLOT), view(name, LAND + SLOT * k, LAND + SLOT * (k + 1)))
                       for d, en, k in slots])
            continue
        for p, w in call:
            wait(g, seen, [p + "2"] if w == "r" else {"a": ["qa"], "b": ["qb"], "s": ["qa", "qb"]}[p])
        send(*[(ways[w][0], ways[w][1], p + str(ways[w][3]), piece(p, ways[w][2]), piece(p, ways[w][3])) for p, w in call])
    g.wait_ge(S.sent, sent[0])
